import numpy as np, ml_dtypes
CORES = [13,21,141,149]
N = 4
BF = ml_dtypes.bfloat16
W, K, RO = 3584, 128, 3
M = N * K
def rows(rng, n):
    return np.argsort(rng.random(n.shape + (16,)), axis=-1) < n[..., None]
def swaps(rng, q, k):
    u = np.argsort(rng.random((k.size, 2, 8)), axis=-1) < k[:, None, None]
    a = np.zeros((k.size, 16), bool); a[:, q] = u[:, 0]; a[:, ~q] = u[:, 1]
    return a
def off(rng, q, lo, hi):
    e = rng.integers(lo, hi, q.shape); up = rng.random(q.shape) < 0.5
    return np.where((up & (q + e <= 63)) | (q - e < 0), q + e, q - e)
def mix(rng, q, far, lo, hi):
    y = np.broadcast_to(q, far.shape + (16,))
    return np.where(rows(rng, far), off(rng, y, lo, hi), y)
def put(x, r, g, p, v):
    x[r, g, 2 * p] = v; x[r, g, 2 * p + 1] = v
def names(rng, lim=W // 2):
    p = np.argsort(rng.random((8, 16, W // 2)) + 2.0 * (np.arange(W // 2) >= lim), axis=-1)[..., :M]
    return np.ascontiguousarray((2 * p + rng.integers(0, 2, p.shape)).reshape(8, 16, N, K).transpose(2, 0, 1, 3))
def spots(rng, pairs, alike):
    p = np.repeat(pairs[:, None], 16, axis=1); q = np.take_along_axis(p, np.argsort(rng.random(p.shape), axis=-1), -1)
    for g in alike: q[g] = p[g]
    return np.ascontiguousarray((2 * q + rng.integers(0, 2, q.shape)).transpose(2, 0, 1, 3))
def lay(pairs, rec, rest):
    z = rest.copy()
    for g in range(8): z[:, g, pairs[g].reshape(-1)] = rec[:, g]
    return np.repeat(z, 2, axis=2)
def near(rng, a, p, amp=1):
    a = np.broadcast_to(a, (N, 8, W, 16)); e = np.where(rng.random(a.shape) < 0.5, 1, rng.integers(2, 6, a.shape)) * (2 * rng.integers(0, 2, a.shape) - 1)
    return np.clip(a + amp * e * (rng.random(a.shape) < p), 0, 63)
def pack(fa, cl, ru):
    b = np.ascontiguousarray(ru.transpose(0, 2, 1)).reshape(128, 16).astype(np.float32).astype(BF)
    return {"fa": np.ascontiguousarray(fa.transpose(0, 1, 3, 2)).reshape(N, 128, W).astype(np.float32).astype(BF),
            "cl": np.ascontiguousarray(cl).reshape(N, 128, K).astype(np.int32), "ru": np.stack([b] * N)}
def setup_inputs(rng):
    a = rng.integers(1, 63, (8, 16)); e = (rng.random((N, 8, 16)) < 0.12) * (2 * rng.integers(0, 2, (N, 8, 16)) - 1)
    fa = near(rng, (a + e)[:, :, None], 0.3 + 0.6 * rng.random((N, 8, W, 1)))
    ru = np.clip(a[:, None] + (rng.random((8, 16, 16)) < 0.1) * (2 * rng.integers(0, 2, (8, 16, 16)) - 1), 0, 63)
    return pack(fa, names(rng), ru)
def setup_inputs_spread(rng):
    a = rng.integers(0, 64, (1, 8, 1, 16)); e = (rng.random((N, 8, 1, 16)) < 0.12) * (2 * rng.integers(0, 2, (N, 8, 1, 16)) - 1)
    fa = near(rng, np.clip(a + e, 0, 63), rng.random((N, 8, W, 1)) ** 2 + 0.1, 2 ** rng.integers(0, 5, (N, 8, W, 1)))
    s = np.where(rng.random((N, 4, W, 1)) < 0.6, 16, rng.choice(np.array([1, 3, 8]), (N, 4, W, 1)))
    u = np.minimum((64 * rng.random((N, 4, W, 16)) ** s).astype(np.int64), 63)
    fa[:, 1::2] = np.where(rng.random((1, 4, 1, 16)) < 0.5, 63 - u, u)
    ru = fa[rng.integers(0, N, (8, 16)), np.arange(8)[:, None], rng.integers(0, W, (8, 16))]
    cl = names(rng, rng.choice(np.array([M, M + M // 2, W // 2]), (8, 16, 1))); cl[:, 4:] = W - 1 - cl[:, 4:]
    return pack(fa, cl, ru)
def setup_inputs_ends(rng):
    h = M // 2; s = np.concatenate([np.arange(h), np.arange(W // 2 - h, W // 2)]); o = np.stack([rng.permutation(s) for g in range(8)])
    for g in (1, 3, 5, 7):
        j = int(np.argmax(o[g])); o[g, j] = o[g, M - 1]; o[g, M - 1] = W // 2 - 1
    pairs = o.reshape(8, N, K); cl = spots(rng, pairs, (1, 3, 5, 7)); cl[N - 1, 7, :, K - 1] = W - 1
    q = np.argsort(rng.random((N, 8, 16)), axis=-1) < 8; q[:, 2] = q[0, 2].copy(); q[:, 6] = q[0, 6].copy()
    n = rng.integers(0, 7, (N, 8, M)); n[:, 3] = rng.integers(1, 7, (N, M)); n[:, 7] = rng.integers(1, 7, (N, M))
    n[:, 3, M - 2:] = 0; n[:, 7, M - 1] = 0
    for g in (2, 6):
        for r in range(N - 1): n[r, g, r * K + int(rng.integers(0, K))] = 8
    flip = rows(rng, n); rec = 63 * (q[:, :, None] ^ flip).astype(np.int64)
    for g in (0, 1, 4, 5):
        for r in range(N):
            if g % 4 == 0:
                k = rng.integers(0, 4, h); k[0] = 0; a = swaps(rng, q[r, g], k)
            else:
                a = flip[r, g, :h].copy(); a[0] = False
            e = a[rng.permutation(h)]
            if g % 4 == 1: a, e = np.concatenate([a, a[:1]]), a[1:]
            t = np.concatenate([q[r, g] ^ a, ~q[r, g] ^ e]); v = 63 * t.astype(np.int64)
            if g % 4 == 0:
                u = rows(rng, rng.integers(0, 8, M)).astype(np.int64); u = u[:, :8] + u[:, 8:]; u[0] = 1; v[~t] = u.reshape(-1)
            rec[r, g] = np.concatenate([v[1:][rng.permutation(M - 1)], v[:1]])
    ru = np.stack([q[k % N] if k % 5 != 4 else ~q[0] for k in range(16)], axis=1)
    rest = 63 * (rng.random((N, 8, W // 2, 16)) < 0.5).astype(np.int64)
    return pack(lay(pairs, rec, rest), cl, 63 * ru.astype(np.int64))
def setup_inputs_corners(rng):
    o = np.stack([rng.permutation(M) for g in range(8)]); o[0] = np.arange(M); o[1] = np.arange(M)[::-1]
    o[1::2] += W // 2 - M; pairs = o.reshape(8, N, K); cl = spots(rng, pairs, ())
    bit = rng.integers(0, 2, (8, N, K)); bit[0] = 0; bit[1] = 1
    for g in (0, 1, 2, 3, 6, 7): cl[:, g] = (2 * pairs[g] + bit[g])[:, None]
    q = np.repeat(rng.choice(np.array([0, 1, 31, 32, 62, 63]), (1, 8, 16)), N, axis=0)
    q = np.where(rows(rng, np.full((N, 8), 2)), off(rng, q, 1, 4), q)
    x = np.repeat(q[:, :, None], W, axis=2); far = rng.integers(3, 6, (N, 8, W, 1)); eq = rng.integers(8, 11, (N, 8, W, 1))
    pos = np.argsort(rng.random(x.shape), axis=-1)
    x = np.where(pos < far, off(rng, x, 2, 3), np.where(pos < 16 - eq, off(rng, x, 1, 2), x))
    x = np.where(rng.random((N, 8, W, 1)) < 0.125, rng.integers(0, 64, x.shape), x)
    x[:, 4:] = np.where(rng.random((N, 4, W, 1)) < 0.03, q[:, 4:, None], x[:, 4:])
    for g, js in ((0, (0,)), (1, (M - 1,)), (2, (M - 2, M - 1)), (3, (K, M - 1))):
        for j in js: x[:, g, int(cl[:, g, 0].reshape(-1)[j])] = q[:, g]
    return pack(x, cl, np.stack([q[k % N] for k in range(16)], axis=1))
def camps(rng, q, n):
    pairs = np.stack([rng.permutation(W // 2)[:M] for g in range(8)]).reshape(8, N, K)
    far = rng.integers(0, 7, (N, 8, N, K)); u = np.argsort(rng.random((N, 8, K)), axis=-1)
    for r in range(N):
        far[r, :, r] = np.where(u[r] < n[:, r, None], 7, 8); far[r, :, (r + 1) % N, K - 1] = 0
    x = np.broadcast_to(q[None, :, None, None], (N, 8, N, K, 16)); rec = np.where(rows(rng, far), off(rng, x, 2, 8), x).reshape(N, 8, M, 16)
    y = np.broadcast_to(q[None, :, None], (N, 8, W // 2, 16)); rest = np.where(rows(rng, rng.integers(0, 7, (N, 8, W // 2))), off(rng, y, 2, 8), y)
    t = np.repeat(q[:, None], 16, axis=1); v = np.where(rows(rng, np.full((8, 16), 2)), off(rng, t, 1, 2), t)
    return lay(pairs, rec, rest), spots(rng, pairs, ()), np.where((np.arange(16) % 2 == 0)[None, :, None], t, v)
def setup_inputs_crowd(rng):
    n = K - rng.integers(0, 2, (8, N)); n[0] = K - 1; n[0, N - 1] = K; n[1] = K; n[2] = 0; n[3] = 0; n[3, 0] = K; n[7] = K; n[7, 0] = K - 1
    q = rng.integers(0, 4, (8, 16)); q[::2] += 60
    x, cl, ru = camps(rng, q, n)
    p = rng.permutation(np.setdiff1d(np.arange(W // 2), cl[:, 1] >> 1))[:M].reshape(N, K)
    cl[:, 1, 16 - N:] = (2 * p + rng.integers(0, 2, p.shape))[:, None]; ru[1, 16 - N:] = q[1]
    for r in range(N):
        far = rng.integers(0, 7, (N, K)); far[0] = rng.integers(0, 5, K); far[r] = 7; far[(r + 1) % N, K - 1] = 0
        v = mix(rng, q[1], far, 2, 8)
        if r == 0:
            u = np.argsort(rng.random((K, 16)), axis=-1); y = np.broadcast_to(q[1], (K, 16))
            v[0] = np.where(u < rng.integers(0, 5, (K, 1)), off(rng, y, 2, 8), np.where(u < 8, off(rng, y, 1, 2), y))
        put(x, r, 1, p, v)
    p = cl[:, 4, 0] >> 1
    for r in range(N):
        far = rng.integers(0, 5, (N, K)); far[(r + 1) % N, K - 1] = 0
        put(x, r, 4, p, mix(rng, q[4], far, 2, 8))
    p = cl[:, 5, 0] >> 1; s = rng.integers(0, 2, W // 2); cl[:, 5] = 2 * (cl[:, 5] >> 1) + s[cl[:, 5] >> 1]
    for r in range(N):
        far = rng.integers(5, 7, (N, K)); far[(r + 1) % N, K - 1] = 0; x[r, 5, 2 * p + s[p]] = mix(rng, q[5], far, 2, 8)
        far = rng.integers(1, 5, (N, K)); far[(r + 1) % N, K - 1] = 0; x[r, 5, 2 * p + 1 - s[p]] = mix(rng, q[5], far, 16, 32)
    p = (cl[:, 6, 0] >> 1).reshape(M); low = q[6] - rng.integers(8, 16, 16)
    for r in range(N):
        v = np.repeat(np.stack([q[6], low]), M // 2, axis=0)
        v = np.clip(v + rows(rng, np.full(M, 2)) * np.where(np.arange(M) < M // 2, 1, -1)[:, None], 0, 63)
        e = rng.permutation(16)[:(4, 12)[r % 2]]; v[rng.permutation(M // 2)[:e.size], e] = low[e]
        put(x, r, 6, p, v)
    return pack(x, cl, ru)
def setup_inputs_calm(rng):
    n = rng.integers(0, 4, (8, N))
    for g in (0, 2, 4, 6): n[g] = rng.permutation(N) % 4
    q = rng.integers(0, 4, (8, 16)); q[1::2] += 60
    return pack(*camps(rng, q, n))
def check_inputs(d):
    bad = []
    for k, lo, hi in (("fa", 0, 63), ("cl", 0, W - 1), ("ru", 0, 63)):
        v = np.asarray(d[k], np.float64)
        if not (np.min(v) >= lo and np.max(v) <= hi): bad.append("range of " + k)
        elif np.any(v != np.floor(v)): bad.append("whole numbers of " + k)
    v = np.asarray(d["ru"], np.float64)
    if np.any(v != v[:1]): bad.append("ru alike on all ranks")
    p = (np.asarray(d["cl"]).astype(np.int64) >> 1).reshape(N, 8, 16, K).transpose(1, 2, 0, 3).reshape(8, 16, M)
    p = np.sort(p, axis=-1)
    if np.any(p[..., 1:] == p[..., :-1]): bad.append("pairs of cl differ in a group and issue")
    return bad
def reference(fa, cl, ru):
    x = np.ascontiguousarray(np.asarray(fa, np.float32).astype(np.int64).reshape(N, 8, 16, W).transpose(0, 1, 3, 2))
    c = cl.astype(np.int64).reshape(N, 8, 16, K)
    b = np.asarray(ru[0], np.float32).astype(np.int64).reshape(8, 16, 16).transpose(0, 2, 1).copy()
    g8 = np.arange(8)[:, None]
    for rnd in range(RO):
        vote = np.zeros((N, 8, 16), np.int64)
        for r in range(N):
            z = x[r][g8[:, :, None], c[r]]
            eq = np.add.reduce((z == b[:, :, None]).astype(np.int64), axis=3)
            vote[r] = np.add.reduce((eq >= 9).astype(np.int64), axis=2)
        court = np.zeros((8, 16), np.int64)
        for g in range(8):
            taken = np.zeros(N, bool)
            for k in range(16):
                if k % N == 0: taken = np.zeros(N, bool)
                court[g, k] = np.argmax(np.where(taken, -1, vote[:, g, k])); taken[court[g, k]] = True
        up = np.zeros((N, 8, 16, K), bool)
        for k in range(16):
            r = court[:, k][:, None]; nm = c[:, :, k].transpose(1, 0, 2).reshape(8, M)
            z = x[r, g8, nm]
            med = np.sort(z, axis=1)[:, M // 2]
            dist = np.add.reduce(np.abs(z - med[:, None]), axis=2)
            b[:, k] = z[np.arange(8), np.argmin(dist, axis=1)]
            diff = b[:, k][:, None] - z
            ok = np.add.reduce((np.abs(diff) <= 1).astype(np.int64), axis=2) >= 12
            x[r, g8, nm] = z + np.where(ok[..., None], np.sign(diff), 0)
            up[:, :, k] = ok.reshape(8, N, K).transpose(1, 0, 2)
        c = np.where(up, c, c ^ 1)
    yb = np.ascontiguousarray(b.transpose(0, 2, 1)).reshape(128, 16).astype(np.float32).astype(BF)
    return {"yf": np.ascontiguousarray(x.transpose(0, 1, 3, 2)).reshape(N, 128, W).astype(np.float32).astype(BF), "yc": c.reshape(N, 128, K).astype(np.float32), "yr": np.stack([yb] * N)}

@@ -1,0 +1,653 @@
+from concourse.bass import DstId, RemoteDMATransfer
+from concourse.mybir import AluOpType as ALU, AxisListType as AX, ActivationFunctionType as AF
+
+W, RO, NR = 3584, 3, 4
+WIN = 49152
+BIGW = 65536.0
+RND128 = 1610612736.0
+RND2 = 25165824.0
+RND4 = 50331652.0
+RS = 960
+LP, LQ = 320, 800
+OKB = (0, 160, 480, 640)
+
+F, B, I, U = "float32", "bfloat16", "int32", "uint16"
+SCRATCH = {
+    "tab": ("sbuf", [128, WIN], B),
+    "cli": ("sbuf", [128, 128], I), "tin": ("sbuf", [128, 288], F), "tout": ("sbuf", [128, 288], F),
+    "ru0": ("sbuf", [128, 16], B), "rug": ("sbuf", [128, 96], B), "ruo": ("sbuf", [128, 16], B),
+    "cu": ("sbuf", [128, 512], U), "ci": ("sbuf", [128, 512], I), "cj": ("sbuf", [128, 512], I),
+    "name": ("sbuf", [128, 512], F), "base": ("sbuf", [128, 512], F), "bit": ("sbuf", [128, 2048], B),
+    "offv": ("sbuf", [128, 128], U), "eq": ("sbuf", [128, 2048], B), "ab": ("sbuf", [128, 640], B),
+    "vt": ("sbuf", [128, 96], F), "res": ("sbuf", [128, RO * RS], B), "wi": ("sbuf", [128, 160], I),
+    "wj": ("sbuf", [128, 480], I), "un": ("sbuf", [128, 320], B),
+    "sc": ("sbuf", [128, 16], F), "pen": ("sbuf", [128, 32], F), "mm": ("sbuf", [128, 32], F),
+    "selb": ("sbuf", [128, 8], F), "selu": ("sbuf", [128, 8], U), "selo": ("sbuf", [128, 256], F),
+    "offs": ("sbuf", [128, 128], U), "offx": ("sbuf", [128, 32], F), "offy": ("sbuf", [128, 32], U),
+    "okof": ("sbuf", [128, 48], U), "ruof": ("sbuf", [128, 4], U),
+    "z": ("sbuf", [128, 512], B), "zs": ("sbuf", [128, 512], B), "ge": ("sbuf", [128, 512], B),
+    "sn": ("sbuf", [128, 256], B), "d1": ("sbuf", [128, 512], B), "d2": ("sbuf", [128, 512], B),
+    "ya": ("sbuf", [128, 512], B), "far": ("sbuf", [128, 512], B), "ua": ("sbuf", [128, 512], B),
+    "junk": ("sbuf", [128, 1024], B), "junq": ("sbuf", [128, 64], F),
+    "ss": ("sbuf", [128, 144], F), "nb": ("sbuf", [128, 16], F), "qq": ("sbuf", [128, 8], F),
+    "sv": ("sbuf", [128, 32], F), "okt": ("sbuf", [128, 32], B),
+    "pi": ("sbuf", [128, 16], I), "pc": ("sbuf", [128, 48], F), "col": ("sbuf", [128, 144], F),
+    "ivw": ("sbuf", [128, 144], F), "ibo": ("sbuf", [128, 128], F), "ism": ("sbuf", [128, 64], F),
+    "vw": ("sbuf", [128, 144], B), "bop": ("sbuf", [128, 128], B), "bon": ("sbuf", [128, 128], B),
+    "idn": ("sbuf", [128, 128], B), "selp": ("sbuf", [128, 144], B), "ones": ("sbuf", [128, 128], B),
+    "idx": ("sbuf", [128, 512], B), "jc": ("sbuf", [128, 64], B), "cf": ("sbuf", [128, 64], F),
+    "lu": ("sbuf", [128, 64], U), "yco": ("sbuf", [128, 128], F),
+    "pk": ("psum", [128, 512], F), "px0": ("psum", [128, 512], F), "px1": ("psum", [128, 512], F),
+    "pv": ("psum", [128, 512], F),
+}
+MSGS = ["cl", "v0", "p0", "q0", "v1", "w1", "p1", "q1", "v2", "w2", "p2", "q2"]
+DMAS = ["d_cl", "d_ru", "d_fa0", "d_fa1", "d_yf0", "d_yf1", "d_yc", "d_yr"]
+SEMAPHORES = ["eV", "eS", "eP", "eG", "sent"] + ["m_" + m for m in MSGS] + DMAS
+
+
+def msg_cols(m, r):
+    if m == "cl":
+        return "cu", 128 * r, 128 * r + 128
+    t = int(m[1])
+    if m[0] in "vw":
+        a = 32 * t + (16 if m[0] == "w" else 0) + 4 * r
+        return "vt", a, a + 4
+    a = RS * t + (LP if m[0] == "p" else LQ) + 40 * r
+    return "res", a, a + 36
+
+
+def routes(T, topo):
+    out = {}
+    for r, c in enumerate(T.cores):
+        direct, via, used = [], [], []
+        for s, d in enumerate(T.cores):
+            if s == r:
+                continue
+            if topo.may_write(c, d):
+                direct.append(s)
+                continue
+            cand = [h for h in topo.cores_of(c) if h != c and h not in T.cores and h not in used and topo.may_write(h, d)]
+            cand.sort(key=lambda h: topo.die(h) != topo.die(c))
+            used.append(cand[0])
+            via.append((cand[0], s))
+        out[r] = (direct, via)
+    return out
+
+
+def mask_of(engs):
+    m = 0
+    for e in engs:
+        m |= 1 << e
+    return m
+
+
+def helper_program(g, core, src, dst, T, topo, n_in):
+    d = T.cores[dst]
+    rid, pid = topo.addr(d, core)
+    eng = topo.engines(core, d)
+    for m in MSGS:
+        buf, a, b = msg_cols(m, src)
+        g.wait_ge(T.sem["m_" + m], n_in)
+        g.remote_dma(T[buf][:, a:b], T[buf][:, a:b], T.sem["m_" + m], T.sem.sent, pid, rid, mask_of(eng))
+    g.wait_ge(T.sem.sent, len(eng) * len(MSGS))
+
+
+def rank_program(g, core, T, topo):
+    rts = routes(T, topo)
+    me = T.rank_of(core)
+    if me is None:
+        for r, (direct, via) in rts.items():
+            far = topo.engines(T.cores[r], T.cores[direct[0]])
+            for h, s in via:
+                if h == core:
+                    helper_program(g, core, r, s, T, topo, len(far))
+        return
+    rank_code(g, core, me, T, topo, rts)
+
+
+def rank_code(g, core, me, T, topo, rts):
+    ops = []
+
+    def A(n, a=0, b=None, s=1, p=None):
+        b = SCRATCH[n][1][1] if b is None else b
+        ap = T[n][:, a:b:s] if s != 1 else T[n][:, a:b]
+        if p is not None:
+            ap = T[n][p[0]:p[1], a:b]
+        if SCRATCH[n][0] == "psum":
+            return (ap, [(n, 0, 1 << 20)])
+        return (ap, [(n, a, b)])
+
+    def X(w, o):
+        return (w[0].indirect(o[0]), w[1], o[1])
+
+    def rd(*xs):
+        out = []
+        for x in xs:
+            if isinstance(x, tuple):
+                out += x[1]
+                if len(x) == 3:
+                    out += x[2]
+        return out
+
+    def v(x):
+        return x[0] if isinstance(x, tuple) else x
+
+    def add(q, call, out, ins, ev=None):
+        r = rd(*ins)
+        w = []
+        for o in out:
+            w += o[1]
+            if len(o) == 3:
+                r += o[2]
+        ops.append([q, call, r, w, ev])
+
+    def ts(o, i, s1, op0, s2=None, op1=None):
+        if op1 is None:
+            add("V", lambda: g.vector.tensor_scalar(v(o), v(i), v(s1), None, op0), [o], [i, s1])
+        else:
+            add("V", lambda: g.vector.tensor_scalar(v(o), v(i), v(s1), v(s2), op0, op1), [o], [i, s1, s2])
+
+    def tt(o, a, b, op):
+        add("V", lambda: g.vector.tensor_tensor(v(o), v(a), v(b), op), [o], [a, b])
+
+    def cp(o, i):
+        add("V", lambda: g.vector.tensor_copy(v(o), v(i)), [o], [i])
+
+    def ms(o, c):
+        add("V", lambda: g.vector.memset(v(o), c), [o], [])
+
+    def red(o, i, op, neg=False):
+        add("V", lambda: g.vector.tensor_reduce(v(o), v(i), AX.X, op, negate=neg), [o], [i])
+
+    def turn():
+        add("V", lambda: g.vector.transpose(T.tout[:], T.tin[:]), [A("tout")], [A("tin")])
+
+    def act(o, i, f, bias=0.0, scale=1.0, acc=None):
+        outs = [o] + ([acc] if acc is not None else [])
+        if acc is None:
+            add("S", lambda: g.scalar.activation(v(o), v(i), f, bias=v(bias), scale=v(scale)), outs, [i, bias, scale])
+        else:
+            add("S", lambda: g.scalar.activation(v(o), v(i), f, bias=v(bias), scale=v(scale), accum_out=v(acc)),
+                outs, [i, bias, scale])
+
+    def mm(o, l, r, st, sp):
+        add("P", lambda: g.tensor.matmul(v(o), v(l), v(r), st, sp), [o], [l, r])
+
+    def iota(o, pat, base=0, cm=0, flt=True):
+        if flt:
+            add("G", lambda: g.iota(v(o), pat, base, cm, allow_small_or_imprecise_dtypes=True), [o], [])
+        else:
+            add("G", lambda: g.iota(v(o), pat, base, cm), [o], [])
+
+    def dma(q, o, i, sem):
+        eng = g.sync if q == "Y" else g.scalar
+        add(q, lambda: eng.dma_start(v(o), v(i)), [o] if isinstance(o, tuple) else [], [i], ("dma", sem, 16))
+
+    direct, via = rts[me]
+    far = topo.engines(core, T.cores[direct[0]])
+    n_sent = [0]
+
+    def send(m):
+        s = A(*msg_cols(m, me))
+        trs = []
+        for j, (h, _) in enumerate(via):
+            spare = [e for e in topo.engines(core, h) if e not in far]
+            eng = spare if j == 0 else far
+            rid, pid = topo.addr(h, core)
+            trs.append(RemoteDMATransfer(dst_ids=[DstId(rid=rid, pnc=pid)], dma_engine_mask=mask_of(eng[:len(far)]),
+                                         remote_sem=T.sem["m_" + m], src=s[0], dst=s[0]))
+            n_sent[0] += len(far)
+        add("G", lambda: g.remote_dma_fused(trs, local_sem=T.sem.sent), [], [s], ("send",))
+        for r in direct:
+            rid, pid = topo.addr(T.cores[r], core)
+            n_sent[0] += len(far)
+            add("G", lambda rid=rid, pid=pid: g.remote_dma(s[0], s[0], T.sem["m_" + m], T.sem.sent, pid, rid, mask_of(far)),
+                [], [s], ("send",))
+
+    def arrive(m):
+        w = [A(*msg_cols(m, r)) for r in range(NR) if r != me]
+        add("X", None, w, [], ("ext", "m_" + m, len(far) * (NR - 1)))
+
+    def c1(n, j):
+        return A(n, j, j + 1)
+
+    spare_work = []
+
+    def later(steps):
+        spare_work.extend(steps)
+
+    def fill(n=1):
+        for _ in range(n):
+            if spare_work:
+                spare_work.pop(0)()
+
+    SIGN, IDT, ABS, RELU = AF.Sign, AF.Identity, AF.Abs, AF.Relu
+    TAB = A("tab", 0, W)
+    own = (128 * me, 128 * me + 128)
+    others = [x for x in ((0, own[0]), (own[1], 512)) if x[1] > x[0]]
+
+    dma("Y", A("cli"), T.cl[:], "d_cl")
+    dma("S", A("ru0"), T.ru[:], "d_ru")
+    half = W // 2
+    dma("Y", A("tab", 0, half), T.fa[:, 0:half], "d_fa0")
+    dma("S", A("tab", half, W), T.fa[:, half:W], "d_fa1")
+
+    P_, p_, g_, h_, b_, x_, u_, e_, o_, y_ = [c1("pc", j) for j in range(10)]
+    kap, g16, vo, so, jo, h16, t0, t1, t2, t3, t4, t5, t6, t7 = [c1("pc", j) for j in range(16, 30)]
+    okA, okB, okL, ruA, ruB, ruL = [c1("pc", j) for j in range(32, 38)]
+    ms(A("tin", 128, 144), 0.0)
+    ms(A("tin", 272, 288), 0.0)
+    ms(A("idx", p=(0, 64)), 0.0)
+    iota(c1("pi", 0), [[0, 1]], 0, 1, False)
+    iota(A("ism", 0, 8), [[32, 4], [160, 2]])
+    iota(A("ism", 8, 16), [[0, 4], [-288, 2]], 144)
+    iota(A("col"), [[1, 144]])
+    iota(A("ivw"), [[1, 9], [0, 4], [1000, 4]], -3000)
+    iota(A("ibo"), [[1, 8], [0, 16]])
+    iota(A("ism", 16, 24), [[32, 4], [0, 2]])
+    iota(A("ism", 24, 34), [[32, 5], [0, 2]], -16)
+    iota(A("ism", 40, 56), [[-1, 4], [0, 4]], 3)
+    for j, (sh, an) in enumerate(((0, 15), (4, 7), (4, 1), (0, 3), (2, 3), (3, 1), (0, 7), (0, 1), (1, 1))):
+        ts(c1("pi", 1 + j), c1("pi", 0), sh, ALU.logical_shift_right, an, ALU.bitwise_and)
+    cp(A("pc", 0, 10), A("pi", 0, 10))
+    FF = A("cf", 0, 8)
+    ts(FF, A("ism", 8, 16), h_, ALU.mult)
+    ts(kap, b_, 4.0, ALU.mult, x_, ALU.add)
+    ts(vo, e_, 16.0, ALU.mult, u_, ALU.add)
+    tt(FF, FF, A("ism", 0, 8), ALU.add)
+    L_FW, L_VO, L_OUT, L_YY, L_B5, L_B6, L_KP = (A("lu", 0, 8), A("lu", 8, 16), A("lu", 16, 24), A("lu", 24, 42),
+                                                 A("lu", 42, 44), A("lu", 44, 48), A("lu", 48, 49))
+    ts(L_VO, A("col", 0, 8), 2.0, ALU.mult, vo, ALU.add)
+    ts(L_FW, FF, kap, ALU.add)
+    ts(A("vw"), A("ivw"), g_, ALU.is_equal)
+    cp(A("tin", 0, 128), A("cli"))
+    cp(A("tin", 144, 272), A("cli"))
+    turn()
+    cp(A("cu", *own), X(A("tout"), L_FW))
+    send("cl")
+    iota(A("idx", p=(0, 1)), [[128, 512]], -32768)
+    cp(A("name", *own), A("cu", *own))
+    cp(A("offv"), X(A("name", *own), L_VO))
+    ms(A("res"), 0.0)
+
+    def late_constants():
+        ms(A("idx", p=(32, 33)), -255.0 * BIGW)
+        ms(A("ones"), 1.0)
+        ms(A("ss"), -0.5)
+        ms(A("jc", 32, 64), -16640.0)
+        ms(A("lu", 42, 46), 0)
+        ts(g16, g_, 16.0, ALU.mult, 15.0, ALU.add)
+        ts(jo, p_, -256.0, ALU.add)
+        ts(t0, x_, 16.0, ALU.mult, b_, ALU.add)
+        ts(h16, h_, 16.0, ALU.mult)
+        ts(t1, p_, 8.0, ALU.is_ge, 1.0, ALU.add)
+        ts(t4, p_, 15.0, ALU.is_ge, 3.0, ALU.mult)
+        ts(A("cf", 16, 32), A("ism", 40, 56), 0.25, ALU.mult)
+        ts(A("cf", 32, 36), A("col", 0, 4), x_, ALU.is_equal)
+        ts(so, t0, 12.0, ALU.add, 128.0, ALU.mult)
+        ts(t2, p_, 12.0, ALU.is_ge, t1, ALU.add)
+        ts(A("bop"), A("ibo"), g_, ALU.is_equal, BIGW, ALU.mult)
+        ts(A("bon"), A("ibo"), g_, ALU.is_equal, -BIGW, ALU.mult)
+        ts(A("idn"), A("col", 0, 128), P_, ALU.is_equal)
+        ts(A("selp"), A("col"), g16, ALU.is_equal, 4096.0, ALU.mult)
+        ts(A("jc", 0, 32), A("col", 0, 32), 16.0, ALU.mult, jo, ALU.add)
+        ts(A("cf", 8, 16), A("col", 0, 8), 8192.0, ALU.mult, so, ALU.add)
+        ts(t3, p_, 14.0, ALU.is_ge, t2, ALU.add)
+        ts(L_OUT, FF, p_, ALU.add)
+        ts(A("ism", 16, 34), A("ism", 16, 34), h16, ALU.add, 0.0, ALU.max)
+        ms(A("lu", 46, 47), 1)
+        ts(A("lu", 43, 44), t3, t4, ALU.add)
+        ts(A("lu", 47, 48), t3, t4, ALU.add, 1.0, ALU.add)
+        ts(L_YY, A("ism", 16, 34), 112.0, ALU.min, kap, ALU.add)
+        cp(L_KP, kap)
+        ts(okA, b_, 1.0, ALU.is_equal, 160.0, ALU.mult)
+        ts(t5, b_, y_, ALU.add, 160.0, ALU.mult)
+        ts(t6, b_, 3.0, ALU.is_equal, 160.0, ALU.mult)
+        ts(ruA, o_, LP + 32.0, ALU.add)
+        ts(t7, b_, 3.0, ALU.is_equal, LQ - LP - 3.0, ALU.mult)
+        cp(okB, t5)
+        tt(okL, t5, t6, ALU.add)
+        ts(ruB, y_, float(LQ - LP), ALU.mult, ruA, ALU.add)
+        ts(ruL, b_, LP + 32.0, ALU.add, t7, ALU.add)
+
+    PB = ["pk", "px0", "px1", "pv"]
+    nstale = [0]
+
+    def votes(t, m, blocks, on_s, ru):
+        todo = [4 * kk + b for kk in range(4) for b in blocks]
+        for j, k in enumerate(on_s):
+            act(A("ab", 128 * j, 128 * j + 128), X(TAB, A("offv", 8 * k, 8 * k + 8)), ABS, ru(k), -1.0)
+        j = 0
+        while j < len(on_s):
+            n = 1
+            while j + n < len(on_s) and on_s[j + n] == on_s[j] + n:
+                n += 1
+            act(A("eq", 128 * on_s[j], 128 * (on_s[j] + n)), A("ab", 128 * j, 128 * (j + n)), RELU, 1.0, -1.0)
+            j += n
+        for k in todo:
+            if k not in on_s:
+                ts(A("eq", 128 * k, 128 * k + 128), X(TAB, A("offv", 8 * k, 8 * k + 8)), ru(k), ALU.is_equal)
+        a = msg_cols(m, me)[1]
+        for kk in (0, 1, 3, 2):
+            order = [b for b in range(max(blocks) + 1) if b not in blocks]
+            order += [b for b in blocks if 4 * kk + b in on_s] + [b for b in blocks if 4 * kk + b not in on_s]
+            for n, b in enumerate(order):
+                k = 4 * kk + b
+                mm(A(PB[kk], 0, 128), A("vw", 3 - b, 131 - b), A("eq", 128 * k, 128 * k + 128), n == 0, n == len(order) - 1)
+            act(A("junk", 128 * kk, 128 * kk + 128), A(PB[kk], 0, 128), SIGN, -8.5, 1.0, c1("vt", a + kk))
+        send(m)
+
+    def courts(m, so_, blocks):
+        a = msg_cols(m, 0)[1]
+        s0, s1, s2 = A("sc", 0, 16, 4), A("sc", 1, 16, 4), A("sc", 2, 16, 4)
+        mx = [c1("mm", j) for j in range(3)]
+        p0, p1, p2, u1, u2, u3 = [A("pen", 4 * j, 4 * j + 4) for j in range(6)]
+        steps = [
+            lambda: (arrive(m), tt(A("sc"), A("vt", a, a + 16), A("cf", 16, 32), ALU.add)),
+            lambda: red(mx[0], s0, ALU.max),
+            lambda: ts(p0, s0, mx[0], ALU.is_equal, -1536.0, ALU.mult),
+            lambda: tt(u1, s1, p0, ALU.add),
+            lambda: tt(u2, s2, p0, ALU.add),
+            lambda: red(mx[1], u1, ALU.max),
+            lambda: ts(p1, u1, mx[1], ALU.is_equal, -1024.0, ALU.mult),
+            lambda: tt(u3, u2, p1, ALU.add),
+            lambda: ts(A("selb"), A("cf", 8, 16), c1("pen", me), ALU.add, c1("pen", 4 + me), ALU.add),
+            lambda: red(mx[2], u3, ALU.max),
+            lambda: ts(c1("pen", 8), c1("pen", 20 + me), mx[2], ALU.is_equal, -512.0, ALU.mult),
+            lambda: ts(A("selu"), A("selb"), c1("pen", 8), ALU.add, 1.0 / 128, ALU.mult),
+            lambda: cp(A("selo", so_, so_ + 128), X(A("name"), A("selu"))),
+        ]
+        for b in blocks:
+            steps.append(lambda b=b: cp(A("offs", 32 * b, 32 * b + 32), A("selo", so_ + b, so_ + 128, 4)))
+        return steps
+
+    def court_lists(t):
+        c40 = c1("mm", 21)
+        steps = [
+            lambda: ts(A("mm", 4, 7), A("mm", 0, 3), RND2, ALU.add, RND2, ALU.subtract),
+            lambda: tt(A("mm", 8, 11), A("mm", 0, 3), A("mm", 4, 7), ALU.subtract),
+            lambda: red(c1("mm", 12), A("mm", 8, 11), ALU.add, True),
+            lambda: ts(c1("mm", 11), c1("mm", 12), 1.5, ALU.add),
+            lambda: tt(A("mm", 16, 20), A("mm", 8, 12), A("cf", 32, 36), ALU.mult),
+            lambda: red(c1("mm", 20), A("mm", 16, 20), ALU.add),
+            lambda: ts(c40, c1("mm", 20), -160.0, ALU.mult, 120.0, ALU.add),
+        ]
+        last = t == RO - 1
+        if not last:
+            steps.append(lambda: ts(A("okof", 32, 40), A("col", 8 * me, 8 * me + 8), c40, ALU.add, okA, ALU.add))
+            steps.append(lambda: ts(c1("ruof", 2), c40, ruA, ALU.add))
+        steps.append(lambda: ts(A("okof", 0, 32), A("col", 0, 32), c40, ALU.add, okL if last else okB, ALU.add))
+        steps.append(lambda: ts(c1("ruof", 0), c40, ruL if last else ruB, ALU.add))
+        return steps
+
+    Z = A("z")
+    JK = A("junk", 512, 1024)
+
+    def count_v(q, w):
+        ts(A("ge"), Z, q, ALU.add, float(w), ALU.is_ge)
+        fill()
+        add("V", lambda: g.vector.tensor_tensor_scan(T.sn[:], T.ge[:, 0:256], T.ge[:, 256:512], -256.0, ALU.add, ALU.add),
+            [A("sn")], [A("ge")])
+
+    def stale_levels(b):
+        n = nstale[0]
+        nstale[0] += 1
+        win = A("ss", 16 * n, 16 * n + 16)
+        for l in range(6):
+            act(JK, A("zs"), SIGN, 0.0 if l == 0 else c1("nb", l), 1.0, c1("ss", 16 * n + l))
+            if l < 5:
+                act(A("junq", 0, 32), X(win, L_B5), SIGN, -0.5, -1.0, c1("nb", l + 1))
+        act(A("junq", 0, 64), X(win, L_B6), SIGN, -0.5, -1.0, c1("nb", 8))
+        act(c1("qq", 2 * b), c1("nb", 8), IDT, -31.0, 0.5)
+        act(c1("qq", 2 * b + 1), c1("nb", 8), IDT, -32.5, 0.5)
+
+    def unpack2(t, m):
+        arrive(m)
+        src, dst = (LP, OKB[0]) if m[0] == "p" else (LQ, OKB[2])
+        w = A("res", RS * t + src, RS * t + src + 160)
+        act(A("un", 0, 160), w, ABS, -1.0)
+        act(A("un", 160, 320), w, RELU, -1.0)
+        act(A("res", RS * t + dst, RS * t + dst + 160), A("un", 0, 160), ABS, -1.0)
+        act(A("res", RS * t + dst + 160, RS * t + dst + 320), A("un", 160, 320), SIGN)
+
+    def unpack3(t):
+        arrive("p%d" % t)
+        cp(A("wi"), A("res", RS * t + LP, RS * t + LP + 160))
+        for b in range(3):
+            ts(A("wj", 160 * b, 160 * b + 160), A("wi"), b, ALU.logical_shift_right, 1, ALU.bitwise_and)
+        cp(A("res", RS * t, RS * t + 320), A("wj", 0, 320))
+        cp(A("res", RS * t + OKB[2], RS * t + OKB[2] + 160), A("wj", 320, 480))
+
+    def rename(t, a, b, win, lst):
+        new = A("bit", 512 * (t + 1) + a, 512 * (t + 1) + b)
+        return [lambda: tt(new, X(win, lst), A("bit", 512 * t + a, 512 * t + b), ALU.is_equal),
+                lambda: tt(A("name", a, b), A("base", a, b), new, ALU.add)]
+
+    def hearing(t, b):
+        last = t == RO - 1
+        off = A("offs", 32 * b, 32 * b + 32)
+        R0 = RS * t
+        px = A("px%d" % (b % 2), 0, 32)
+        pk = A("pk")
+        so_ = 128 if t > 0 and b >= 2 else 0
+        if b == 3:
+            act(A("z", 256, 512), X(TAB, A("offs", 32 * b + 16, 32 * b + 32)), IDT)
+            cp(A("z", 0, 256), X(TAB, A("offs", 32 * b, 32 * b + 16)))
+        else:
+            act(A("zs"), X(TAB, A("offs", 32 * b + 32, 32 * b + 64)), IDT, -31.5)
+            cp(Z, X(TAB, off))
+        mm(pk, A("ones", p=(0, 64)), A("idx", p=(0, 64)), True, False)
+        mm(px, A("idn"), A("jc", 0, 32), True, False)
+        mm(px, A("idn"), A("jc", 32, 64), False, False)
+        mm(pk, A("idn"), Z, False, False)
+        sV, sS = c1("sn", 255), c1("sv", 0)
+        if b == 0:
+            q = -26.5
+            for l, w in enumerate((27, 9, 3)):
+                act(JK, Z, SIGN, q, 1.0, sS)
+                count_v(q, w)
+                bs, aV, aS, qn = c1("sv", 1), c1("sv", 2), c1("sv", 3), c1("sv", 8 + l)
+                if l == 0:
+                    bs = q - float(w + w // 3)
+                else:
+                    ts(bs, q, -float(w + w // 3), ALU.add)
+                ts(aV, sV, 0.0, ALU.is_lt, float(w), ALU.mult)
+                ts(aS, sS, 0.0, ALU.is_lt, float(w), ALU.mult)
+                ts(qn, aS, aV, ALU.add, bs, ALU.add)
+                q = qn
+            qb = c1("sv", 4)
+        else:
+            q, qb = c1("qq", 2 * b), c1("qq", 2 * b + 1)
+        if b == 1:
+            later(court_lists(t))
+        fill()
+        act(JK, Z, SIGN, q, 1.0, sS)
+        count_v(q, 1)
+        if b == 0:
+            ts(qb, q, -1.5, ALU.add)
+        else:
+            fill()
+        nm = c1("sv", 6)
+        ts(c1("sv", 5), sV, 0.0, ALU.is_lt, qb, ALU.add)
+        fill()
+        ts(nm, sS, 0.0, ALU.is_lt, c1("sv", 5), ALU.add)
+        if b == 0:
+            later(courts_rest if t == 0 else courts("w%d" % t, 128, (2, 3)))
+        if b < 3:
+            stale_levels(b + 1)
+            fill()
+            ts(A("d1"), Z, nm, ALU.add, 0.0, ALU.max)
+            ts(A("d2"), Z, nm, ALU.add, 0.0, ALU.min)
+            mm(pk, A("bop"), A("d1"), False, False)
+            mm(pk, A("bon"), A("d2"), False, True)
+        else:
+            act(A("d1", 256, 512), A("z", 256, 512), ABS, nm)
+            ts(A("d2", 0, 256), A("z", 0, 256), nm, ALU.add, 0.0, ALU.min)
+            ts(A("d1", 0, 256), A("z", 0, 256), nm, ALU.add, 0.0, ALU.max)
+            mm(A("pk", 0, 256), A("bon"), A("d2", 0, 256), False, False)
+            mm(pk, A("bop"), A("d1"), False, True)
+            if not last:
+                unpack2(t, "p%d" % t)
+                winA = A("res", R0, R0 + 480)
+                act(A("rug", 32 * t, 32 * t + 16), X(winA, c1("ruof", 2)), IDT)
+        fill(3)
+        key, tq = c1("sv", 12), c1("sv", 13)
+        red(key, pk, ALU.min)
+        fill()
+        ts(tq, key, RND128, ALU.add, RND128, ALU.subtract)
+        fill()
+        inp = b <= (2 if last else 1)
+        j = b if inp else b - (3 if last else 2)
+        slot = R0 + (LP if inp else LQ) + 40 * me
+        rc = slot + 32 + j
+        ts(c1("res", rc), key, tq, ALU.subtract)
+        if b == 3 and not last:
+            later(rename(t, own[0], own[1], winA, A("okof", 32, 40)) + [lambda: cp(A("offv"), X(A("name", *own), L_VO))])
+        else:
+            fill()
+        ts(A("ya"), Z, -1.0, ALU.mult, c1("res", rc), ALU.add)
+        fill()
+        ts(A("far"), A("ya"), RND4, ALU.add, RND4, ALU.not_equal)
+        for p in range(16):
+            mm(px, A("selp", 15 - p, 143 - p), A("far", p, 512, 16), False, p == 15)
+        word = A("res", slot, slot + 32)
+        closes = b == 3 or b == (2 if last else 1)
+        if b == 3:
+            act(A("ua"), A("ya"), SIGN)
+        else:
+            ts(A("ua"), A("ya"), 1.0, ALU.min, -1.0, ALU.max)
+        fill(3)
+        if last and b == 3:
+            ts(word, px, 0.0, ALU.is_lt)
+            send("q%d" % t)
+        tt(A("offx"), px, A("selo", so_ + b, so_ + 128, 4), ALU.max)
+        if last and b == 3:
+            pass
+        elif j == 0:
+            ts(word, px, 0.0, ALU.is_lt)
+        else:
+            ts(A("okt"), px, 0.0, ALU.is_lt, float(2 ** j), ALU.mult)
+        cp(A("offy"), A("offx"))
+        if j > 0:
+            tt(word, word, A("okt"), ALU.add)
+            if closes:
+                send(("p%d" if inp else "q%d") % t)
+        else:
+            fill()
+        tt(X(A("tab"), A("offy")), Z, A("ua"), ALU.add)
+        fill(len(spare_work))
+
+    for t in range(RO):
+        if t == 0:
+            votes(0, "v0", (0, 1, 2, 3), [12, 13, 14, 15, 11], lambda k: c1("ru0", 4 * (k % 4) + k // 4))
+            late_constants()
+            arrive("cl")
+            for a, b in others:
+                cp(A("name", a, b), A("cu", a, b))
+            cp(A("ci"), A("cu"))
+            ts(A("cj"), A("ci"), 1, ALU.bitwise_and)
+            cp(A("bit", 0, 512), A("cj"))
+            tt(A("base"), A("name"), A("bit", 0, 512), ALU.subtract)
+            steps = courts("v0", 0, (0, 1, 2, 3))
+            courts_rest = steps[-2:]
+            steps = steps[:-2]
+        else:
+            votes(t, "v%d" % t, (0, 1), [12, 13], lambda k: c1("rug", 32 * (t - 1) + k))
+            unpack2(t - 1, "q%d" % (t - 1))
+            win = A("res", RS * (t - 1), RS * t)
+            act(A("rug", 32 * t - 16, 32 * t), X(win, c1("ruof", 0)), IDT)
+            for s in rename(t - 1, own[0], own[1], win, A("okof", 8 * me, 8 * me + 8)):
+                s()
+            cp(A("offv"), X(A("name", *own), L_VO))
+            votes(t, "w%d" % t, (2, 3), [14, 15, 11], lambda k: c1("rug", 32 * t - 16 + k))
+            for a, b in others:
+                for s in rename(t - 1, a, b, win, A("okof", a // 16, b // 16)):
+                    s()
+            steps = courts("v%d" % t, 0, (0, 1))
+        for s in steps:
+            s()
+        for b in range(4):
+            hearing(t, b)
+    t = RO - 1
+    dma("Y", T.yf[:, 0:half], A("tab", 0, half), "d_yf0")
+    dma("S", T.yf[:, half:W], A("tab", half, W), "d_yf1")
+    unpack3(t)
+    arrive("q%d" % t)
+    win = A("res", RS * t, RS * t + RS)
+    RU = A("rug", 32 * t, 32 * t + 16)
+    act(RU, X(win, c1("ruof", 0)), IDT)
+    act(A("ruo"), X(RU, L_KP), IDT)
+    dma("S", T.yr[:], A("ruo"), "d_yr")
+    for s in rename(t, own[0], own[1], win, A("okof", 8 * me, 8 * me + 8)):
+        s()
+    cp(A("tin"), X(A("name", *own), L_YY))
+    turn()
+    cp(A("yco"), X(A("tout"), L_OUT))
+    dma("Y", T.yc[:], A("yco"), "d_yc")
+    emit(g, T, ops, n_sent[0])
+
+
+def emit(g, T, ops, n_sent):
+    hist = {}
+    clock = {q: {} for q in "VSPGY"}
+    done = []
+    waits = []
+    marked = set()
+    for n, (q, call, rds, wrs, ev) in enumerate(ops):
+        key = q if ev is None else (None if ev[0] == "send" else ev[1])
+        need = []
+        if q != "X":
+            for (buf, a, b), wr in [(x, False) for x in rds] + [(x, True) for x in wrs]:
+                psum = SCRATCH[buf][0] == "psum"
+                for (m, a2, b2, w2) in hist.get(buf, []):
+                    if a2 < b and a < b2 and (wr or w2 or psum):
+                        same = ops[m][0] == q and ops[m][4] is None
+                        if same and (q == "P" or not (wr or w2)):
+                            continue
+                        if ops[m][4] is not None and ops[m][4][0] == "send":
+                            continue
+                        need.append(m)
+        ws = []
+        ck = clock.get(q, {})
+        for m in sorted(set(need), reverse=True):
+            km = done[m][0]
+            if ck.get(km, -1) >= m:
+                continue
+            ws.append(m)
+            marked.add(m)
+            for k2, v2 in done[m][1].items():
+                if ck.get(k2, -1) < v2:
+                    ck[k2] = v2
+        snap = dict(ck)
+        snap[key] = n
+        done.append((key, snap))
+        waits.append(ws)
+        for x in wrs:
+            if q != "X":
+                hist[x[0]] = [e for e in hist.get(x[0], []) if not (x[1] <= e[1] and e[2] <= x[2])]
+            hist.setdefault(x[0], []).append((n, x[1], x[2], True))
+        for x in rds:
+            hist.setdefault(x[0], []).append((n, x[1], x[2], False))
+    queue = {"V": g.vector, "S": g.scalar, "P": g.tensor, "G": g, "Y": g.sync}
+    count = {q: 0 for q in "VSPG"}
+    value = {}
+    for n, (q, call, rds, wrs, ev) in enumerate(ops):
+        if ev is not None and ev[0] != "send":
+            value[n] = (ev[1], ev[2])
+        elif n in marked:
+            count[q] += 1
+            value[n] = ("e" + q, count[q])
+        if q == "X":
+            continue
+        for m in waits[n]:
+            queue[q].wait_ge(T.sem[value[m][0]], value[m][1])
+        ins = call()
+        if ev is not None and ev[0] == "dma":
+            ins.then_inc(T.sem[ev[1]], 16)
+        elif n in marked:
+            ins.then_inc(T.sem["e" + q], 1)
+    for d in DMAS:
+        g.wait_ge(T.sem[d], 16)
+    for q in "VSPG":
+        g.wait_ge(T.sem["e" + q], count[q])
+    g.wait_ge(T.sem.sent, n_sent)

@@ -8,6 +8,8 @@ RND128 = 1610612736.0
 RND2 = 25165824.0
 RND4 = 50331652.0
 RS = 960
+SPLIT2 = True
+START = 0
 LP, LQ = 320, 800
 OKB = (0, 160, 480, 640)
 
@@ -17,18 +19,19 @@ SCRATCH = {
     "cli": ("sbuf", [128, 128], I), "tin": ("sbuf", [128, 288], F), "tout": ("sbuf", [128, 288], F),
     "ru0": ("sbuf", [128, 16], B), "rug": ("sbuf", [128, 96], B), "ruo": ("sbuf", [128, 16], B),
     "cu": ("sbuf", [128, 512], U), "ci": ("sbuf", [128, 512], I), "cj": ("sbuf", [128, 512], I),
-    "name": ("sbuf", [128, 512], F), "base": ("sbuf", [128, 512], F), "bit": ("sbuf", [128, 2048], B),
+    "name": ("sbuf", [128, 512], F), "base": ("sbuf", [128, 512], I), "bsel": ("sbuf", [128, 128], B),
+    "ub": ("sbuf", [128, 512], B), "bit": ("sbuf", [128, 2048], B),
     "offv": ("sbuf", [128, 128], U), "eq": ("sbuf", [128, 2048], B), "ab": ("sbuf", [128, 640], B),
     "vt": ("sbuf", [128, 96], F), "res": ("sbuf", [128, RO * RS], B), "wi": ("sbuf", [128, 160], I),
     "wj": ("sbuf", [128, 480], I), "un": ("sbuf", [128, 320], B),
     "sc": ("sbuf", [128, 16], F), "pen": ("sbuf", [128, 32], F), "mm": ("sbuf", [128, 32], F),
     "selb": ("sbuf", [128, 8], F), "selu": ("sbuf", [128, 8], U), "selo": ("sbuf", [128, 256], F),
     "offs": ("sbuf", [128, 128], U), "offx": ("sbuf", [128, 32], F), "offy": ("sbuf", [128, 32], U),
-    "okof": ("sbuf", [128, 48], U), "ruof": ("sbuf", [128, 4], U),
+    "okof": ("sbuf", [128, 64], U), "ruof": ("sbuf", [128, 4], U),
     "z": ("sbuf", [128, 512], B), "zs": ("sbuf", [128, 512], B), "ge": ("sbuf", [128, 512], B),
     "sn": ("sbuf", [128, 256], B), "d1": ("sbuf", [128, 512], B), "d2": ("sbuf", [128, 512], B),
     "ya": ("sbuf", [128, 512], B), "far": ("sbuf", [128, 512], B), "ua": ("sbuf", [128, 512], B),
-    "junk": ("sbuf", [128, 1024], B), "junq": ("sbuf", [128, 64], F),
+    "junk": ("sbuf", [128, 1024], B), "junq": ("sbuf", [128, 128], F),
     "ss": ("sbuf", [128, 144], F), "nb": ("sbuf", [128, 16], F), "qq": ("sbuf", [128, 8], F),
     "sv": ("sbuf", [128, 32], F), "okt": ("sbuf", [128, 32], B),
     "pi": ("sbuf", [128, 16], I), "pc": ("sbuf", [128, 48], F), "col": ("sbuf", [128, 144], F),
@@ -40,7 +43,7 @@ SCRATCH = {
     "pk": ("psum", [128, 512], F), "px0": ("psum", [128, 512], F), "px1": ("psum", [128, 512], F),
     "pv": ("psum", [128, 512], F),
 }
-MSGS = ["cl", "v0", "p0", "q0", "v1", "w1", "p1", "q1", "v2", "w2", "p2", "q2"]
+MSGS = ["cl", "v0", "w0", "p0", "q0", "v1", "w1", "p1", "q1", "v2", "w2", "p2", "q2"]
 DMAS = ["d_cl", "d_ru", "d_fa0", "d_fa1", "d_yf0", "d_yf1", "d_yc", "d_yr"]
 SEMAPHORES = ["eV", "eS", "eP", "eG", "sent"] + ["m_" + m for m in MSGS] + DMAS
 
@@ -256,10 +259,18 @@ def rank_code(g, core, me, T, topo, rts):
     ts(vo, e_, 16.0, ALU.mult, u_, ALU.add)
     tt(FF, FF, A("ism", 0, 8), ALU.add)
     L_FW, L_VO, L_OUT, L_YY, L_B5, L_B6, L_KP = (A("lu", 0, 8), A("lu", 8, 16), A("lu", 16, 24), A("lu", 24, 42),
-                                                 A("lu", 42, 44), A("lu", 44, 48), A("lu", 48, 49))
+                                                 A("lu", 42, 44), A("lu", 44, 52), A("lu", 52, 53))
     ts(L_VO, A("col", 0, 8), 2.0, ALU.mult, vo, ALU.add)
     ts(L_FW, FF, kap, ALU.add)
     ts(A("vw"), A("ivw"), g_, ALU.is_equal)
+    ts(okA, b_, 1.0, ALU.is_equal, 160.0, ALU.mult)
+    ts(okB, b_, y_, ALU.add, 160.0, ALU.mult)
+    ts(t6, b_, 3.0, ALU.is_equal, 160.0, ALU.mult)
+    ts(ruA, o_, LP + 32.0, ALU.add)
+    ts(t7, b_, 3.0, ALU.is_equal, LQ - LP - 3.0, ALU.mult)
+    tt(okL, okB, t6, ALU.add)
+    ts(ruB, y_, float(LQ - LP), ALU.mult, ruA, ALU.add)
+    ts(ruL, b_, LP + 32.0, ALU.add, t7, ALU.add)
     cp(A("tin", 0, 128), A("cli"))
     cp(A("tin", 144, 272), A("cli"))
     turn()
@@ -268,6 +279,7 @@ def rank_code(g, core, me, T, topo, rts):
     iota(A("idx", p=(0, 1)), [[128, 512]], -32768)
     cp(A("name", *own), A("cu", *own))
     cp(A("offv"), X(A("name", *own), L_VO))
+    ms(A("vt", 4 * me + 3, 96, 16), 0.0)
     ms(A("res"), 0.0)
 
     def late_constants():
@@ -279,7 +291,6 @@ def rank_code(g, core, me, T, topo, rts):
         ts(g16, g_, 16.0, ALU.mult, 15.0, ALU.add)
         ts(jo, p_, -256.0, ALU.add)
         ts(t0, x_, 16.0, ALU.mult, b_, ALU.add)
-        ts(h16, h_, 16.0, ALU.mult)
         ts(t1, p_, 8.0, ALU.is_ge, 1.0, ALU.add)
         ts(t4, p_, 15.0, ALU.is_ge, 3.0, ALU.mult)
         ts(A("cf", 16, 32), A("ism", 40, 56), 0.25, ALU.mult)
@@ -293,28 +304,28 @@ def rank_code(g, core, me, T, topo, rts):
         ts(A("jc", 0, 32), A("col", 0, 32), 16.0, ALU.mult, jo, ALU.add)
         ts(A("cf", 8, 16), A("col", 0, 8), 8192.0, ALU.mult, so, ALU.add)
         ts(t3, p_, 14.0, ALU.is_ge, t2, ALU.add)
-        ts(L_OUT, FF, p_, ALU.add)
-        ts(A("ism", 16, 34), A("ism", 16, 34), h16, ALU.add, 0.0, ALU.max)
         ms(A("lu", 46, 47), 1)
+        ms(A("lu", 48, 51), 9)
+        ms(A("ss", 9, 144, 16), 0.0)
+        ts(A("lu", 51, 52), p_, 14.0, ALU.is_lt, 8.0, ALU.add)
+        ms(A("cf", 40, 44), 0.0)
+        ms(A("cf", 41, 42), 1.0)
+        ms(A("cf", 43, 44), -3.0)
         ts(A("lu", 43, 44), t3, t4, ALU.add)
         ts(A("lu", 47, 48), t3, t4, ALU.add, 1.0, ALU.add)
-        ts(L_YY, A("ism", 16, 34), 112.0, ALU.min, kap, ALU.add)
+
+    def end_constants():
+        ts(h16, h_, 16.0, ALU.mult)
+        ts(L_OUT, FF, p_, ALU.add)
+        ts(A("ism", 16, 34), A("ism", 16, 34), h16, ALU.add, 0.0, ALU.max)
         cp(L_KP, kap)
-        ts(okA, b_, 1.0, ALU.is_equal, 160.0, ALU.mult)
-        ts(t5, b_, y_, ALU.add, 160.0, ALU.mult)
-        ts(t6, b_, 3.0, ALU.is_equal, 160.0, ALU.mult)
-        ts(ruA, o_, LP + 32.0, ALU.add)
-        ts(t7, b_, 3.0, ALU.is_equal, LQ - LP - 3.0, ALU.mult)
-        cp(okB, t5)
-        tt(okL, t5, t6, ALU.add)
-        ts(ruB, y_, float(LQ - LP), ALU.mult, ruA, ALU.add)
-        ts(ruL, b_, LP + 32.0, ALU.add, t7, ALU.add)
+        ts(L_YY, A("ism", 16, 34), 112.0, ALU.min, kap, ALU.add)
 
     PB = ["pk", "px0", "px1", "pv"]
     nstale = [0]
 
     def votes(t, m, blocks, on_s, ru):
-        todo = [4 * kk + b for kk in range(4) for b in blocks]
+        todo = [4 * kk + b for kk in range(3) for b in blocks]
         for j, k in enumerate(on_s):
             act(A("ab", 128 * j, 128 * j + 128), X(TAB, A("offv", 8 * k, 8 * k + 8)), ABS, ru(k), -1.0)
         j = 0
@@ -328,7 +339,7 @@ def rank_code(g, core, me, T, topo, rts):
             if k not in on_s:
                 ts(A("eq", 128 * k, 128 * k + 128), X(TAB, A("offv", 8 * k, 8 * k + 8)), ru(k), ALU.is_equal)
         a = msg_cols(m, me)[1]
-        for kk in (0, 1, 3, 2):
+        for kk in (0, 2, 1):
             order = [b for b in range(max(blocks) + 1) if b not in blocks]
             order += [b for b in blocks if 4 * kk + b in on_s] + [b for b in blocks if 4 * kk + b not in on_s]
             for n, b in enumerate(order):
@@ -338,6 +349,10 @@ def rank_code(g, core, me, T, topo, rts):
         send(m)
 
     def courts(m, so_, blocks):
+        t = int(m[1])
+        return court_steps(m, so_, blocks, A("bit", 512 * t, 512 * t + 512))
+
+    def court_steps(m, so_, blocks, bits):
         a = msg_cols(m, 0)[1]
         s0, s1, s2 = A("sc", 0, 16, 4), A("sc", 1, 16, 4), A("sc", 2, 16, 4)
         mx = [c1("mm", j) for j in range(3)]
@@ -355,8 +370,12 @@ def rank_code(g, core, me, T, topo, rts):
             lambda: red(mx[2], u3, ALU.max),
             lambda: ts(c1("pen", 8), c1("pen", 20 + me), mx[2], ALU.is_equal, -512.0, ALU.mult),
             lambda: ts(A("selu"), A("selb"), c1("pen", 8), ALU.add, 1.0 / 128, ALU.mult),
-            lambda: cp(A("selo", so_, so_ + 128), X(A("name"), A("selu"))),
         ]
+        if so_:
+            steps.append(lambda: cp(A("bsel"), X(bits, A("selu"))))
+            steps.append(lambda: tt(A("selo", so_, so_ + 128), X(A("base"), A("selu")), A("bsel"), ALU.add))
+        else:
+            steps.append(lambda: cp(A("selo", 0, 128), X(A("name"), A("selu"))))
         for b in blocks:
             steps.append(lambda b=b: cp(A("offs", 32 * b, 32 * b + 32), A("selo", so_ + b, so_ + 128, 4)))
         return steps
@@ -374,7 +393,7 @@ def rank_code(g, core, me, T, topo, rts):
         ]
         last = t == RO - 1
         if not last:
-            steps.append(lambda: ts(A("okof", 32, 40), A("col", 8 * me, 8 * me + 8), c40, ALU.add, okA, ALU.add))
+            steps.append(lambda: ts(A("okof", 32, 64), A("col", 0, 32), c40, ALU.add, okA, ALU.add))
             steps.append(lambda: ts(c1("ruof", 2), c40, ruA, ALU.add))
         steps.append(lambda: ts(A("okof", 0, 32), A("col", 0, 32), c40, ALU.add, okL if last else okB, ALU.add))
         steps.append(lambda: ts(c1("ruof", 0), c40, ruL if last else ruB, ALU.add))
@@ -397,18 +416,21 @@ def rank_code(g, core, me, T, topo, rts):
             act(JK, A("zs"), SIGN, 0.0 if l == 0 else c1("nb", l), 1.0, c1("ss", 16 * n + l))
             if l < 5:
                 act(A("junq", 0, 32), X(win, L_B5), SIGN, -0.5, -1.0, c1("nb", l + 1))
-        act(A("junq", 0, 64), X(win, L_B6), SIGN, -0.5, -1.0, c1("nb", 8))
-        act(c1("qq", 2 * b), c1("nb", 8), IDT, -31.0, 0.5)
-        act(c1("qq", 2 * b + 1), c1("nb", 8), IDT, -32.5, 0.5)
+        act(A("junq"), X(win, L_B6), SIGN, -0.5, -1.0, c1("nb", 8 + b))
 
     def unpack2(t, m):
         arrive(m)
         src, dst = (LP, OKB[0]) if m[0] == "p" else (LQ, OKB[2])
         w = A("res", RS * t + src, RS * t + src + 160)
         act(A("un", 0, 160), w, ABS, -1.0)
-        act(A("un", 160, 320), w, RELU, -1.0)
+        high = A("res", RS * t + dst + 160, RS * t + dst + 320)
+        if m[0] == "p":
+            act(A("un", 160, 320), w, RELU, -1.0)
+        else:
+            ts(high, w, 2.0, ALU.is_ge)
         act(A("res", RS * t + dst, RS * t + dst + 160), A("un", 0, 160), ABS, -1.0)
-        act(A("res", RS * t + dst + 160, RS * t + dst + 320), A("un", 160, 320), SIGN)
+        if m[0] == "p":
+            act(high, A("un", 160, 320), SIGN)
 
     def unpack3(t):
         arrive("p%d" % t)
@@ -429,8 +451,8 @@ def rank_code(g, core, me, T, topo, rts):
         R0 = RS * t
         px = A("px%d" % (b % 2), 0, 32)
         pk = A("pk")
-        so_ = 128 if t > 0 and b >= 2 else 0
-        if b == 3:
+        so_ = 128 if b >= 2 else 0
+        if b != 2 or SPLIT2:
             act(A("z", 256, 512), X(TAB, A("offs", 32 * b + 16, 32 * b + 32)), IDT)
             cp(A("z", 0, 256), X(TAB, A("offs", 32 * b, 32 * b + 16)))
         else:
@@ -446,38 +468,49 @@ def rank_code(g, core, me, T, topo, rts):
             for l, w in enumerate((27, 9, 3)):
                 act(JK, Z, SIGN, q, 1.0, sS)
                 count_v(q, w)
+                if l < 2:
+                    act(A("zs", 256 * l, 256 * l + 256), X(TAB, A("offs", 32 + 16 * l, 48 + 16 * l)), IDT, -31.5)
                 bs, aV, aS, qn = c1("sv", 1), c1("sv", 2), c1("sv", 3), c1("sv", 8 + l)
                 if l == 0:
                     bs = q - float(w + w // 3)
                 else:
                     ts(bs, q, -float(w + w // 3), ALU.add)
-                ts(aV, sV, 0.0, ALU.is_lt, float(w), ALU.mult)
                 ts(aS, sS, 0.0, ALU.is_lt, float(w), ALU.mult)
+                ts(aV, sV, 0.0, ALU.is_lt, float(w), ALU.mult)
                 ts(qn, aS, aV, ALU.add, bs, ALU.add)
                 q = qn
             qb = c1("sv", 4)
+            if START == 0:
+                later(courts("w%d" % t, 128, (2, 3)))
+            fill()
+            act(JK, Z, SIGN, q, 1.0, sS)
         else:
             q, qb = c1("qq", 2 * b), c1("qq", 2 * b + 1)
-        if b == 1:
-            later(court_lists(t))
-        fill()
-        act(JK, Z, SIGN, q, 1.0, sS)
-        count_v(q, 1)
+            ts(A("qq", 2 * b, 2 * b + 2), A("cf", 42, 44), c1("nb", 8 + b), ALU.add, 0.5, ALU.mult)
+            act(JK, Z, SIGN, c1("nb", 8 + b), 2.0, sS)
+            fill()
         if b == 0:
             ts(qb, q, -1.5, ALU.add)
-        else:
-            fill()
-        nm = c1("sv", 6)
-        ts(c1("sv", 5), sV, 0.0, ALU.is_lt, qb, ALU.add)
+        count_v(q, 1)
         fill()
-        ts(nm, sS, 0.0, ALU.is_lt, c1("sv", 5), ALU.add)
-        if b == 0:
-            later(courts_rest if t == 0 else courts("w%d" % t, 128, (2, 3)))
+        if b == 1:
+            fill(len(spare_work) - 1)
+            later(court_lists(t))
+        if b == 1 or (b == 2 and SPLIT2):
+            act(A("zs"), X(TAB, A("offs", 32 * b + 32, 32 * b + 64)), IDT, -31.5)
+        nm = c1("sv", 6)
+        ts(c1("sv", 5), sS, 0.0, ALU.is_lt, qb, ALU.add)
+        fill()
+        ts(nm, sV, 0.0, ALU.is_lt, c1("sv", 5), ALU.add)
         if b < 3:
             stale_levels(b + 1)
+            if b == 0 and START == 1:
+                later(courts("w%d" % t, 128, (2, 3)))
             fill()
             ts(A("d1"), Z, nm, ALU.add, 0.0, ALU.max)
             ts(A("d2"), Z, nm, ALU.add, 0.0, ALU.min)
+            if b == 0 and START == 2:
+                later(courts("w%d" % t, 128, (2, 3)))
             mm(pk, A("bop"), A("d1"), False, False)
             mm(pk, A("bon"), A("d2"), False, True)
         else:
@@ -493,30 +526,30 @@ def rank_code(g, core, me, T, topo, rts):
         fill(3)
         key, tq = c1("sv", 12), c1("sv", 13)
         red(key, pk, ALU.min)
+        if b == 3 and not last:
+            later(rename(t, own[0], own[1], winA, A("okof", 32 + 8 * me, 40 + 8 * me)) + [lambda: cp(A("offv"), X(A("name", *own), L_VO))])
         fill()
         ts(tq, key, RND128, ALU.add, RND128, ALU.subtract)
-        fill()
+        if b < 3:
+            fill()
         inp = b <= (2 if last else 1)
         j = b if inp else b - (3 if last else 2)
         slot = R0 + (LP if inp else LQ) + 40 * me
         rc = slot + 32 + j
-        ts(c1("res", rc), key, tq, ALU.subtract)
-        if b == 3 and not last:
-            later(rename(t, own[0], own[1], winA, A("okof", 32, 40)) + [lambda: cp(A("offv"), X(A("name", *own), L_VO))])
-        else:
-            fill()
-        ts(A("ya"), Z, -1.0, ALU.mult, c1("res", rc), ALU.add)
-        fill()
+        ts(A("ya"), Z, tq, ALU.add, key, ALU.subtract)
+        ts(A("res", rc, rc + 2), A("cf", 40, 42), key, ALU.add, tq, ALU.subtract)
         ts(A("far"), A("ya"), RND4, ALU.add, RND4, ALU.not_equal)
         for p in range(16):
             mm(px, A("selp", 15 - p, 143 - p), A("far", p, 512, 16), False, p == 15)
         word = A("res", slot, slot + 32)
         closes = b == 3 or b == (2 if last else 1)
         if b == 3:
-            act(A("ua"), A("ya"), SIGN)
+            act(A("ua"), A("ya"), SIGN, 0.0, -1.0)
+            fill(3)
         else:
-            ts(A("ua"), A("ya"), 1.0, ALU.min, -1.0, ALU.max)
-        fill(3)
+            ts(A("ua"), Z, 1.0, ALU.add, c1("res", rc), ALU.min)
+            ts(A("ub"), Z, c1("res", rc + 1), ALU.subtract, 0.0, ALU.max)
+            fill()
         if last and b == 3:
             ts(word, px, 0.0, ALU.is_lt)
             send("q%d" % t)
@@ -534,38 +567,42 @@ def rank_code(g, core, me, T, topo, rts):
                 send(("p%d" if inp else "q%d") % t)
         else:
             fill()
-        tt(X(A("tab"), A("offy")), Z, A("ua"), ALU.add)
-        fill(len(spare_work))
+        tt(X(A("tab"), A("offy")), Z if b == 3 else A("ub"), A("ua"), ALU.add)
+        fill(1 if b < 2 else len(spare_work))
 
     for t in range(RO):
         if t == 0:
-            votes(0, "v0", (0, 1, 2, 3), [12, 13, 14, 15, 11], lambda k: c1("ru0", 4 * (k % 4) + k // 4))
+            votes(0, "v0", (0, 1), [8, 9], lambda k: c1("ru0", 4 * (k % 4) + k // 4))
+            votes(0, "w0", (2, 3), [10, 11], lambda k: c1("ru0", 4 * (k % 4) + k // 4))
             late_constants()
             arrive("cl")
             for a, b in others:
                 cp(A("name", a, b), A("cu", a, b))
             cp(A("ci"), A("cu"))
             ts(A("cj"), A("ci"), 1, ALU.bitwise_and)
+            ts(A("base"), A("ci"), 4094, ALU.bitwise_and)
             cp(A("bit", 0, 512), A("cj"))
-            tt(A("base"), A("name"), A("bit", 0, 512), ALU.subtract)
-            steps = courts("v0", 0, (0, 1, 2, 3))
-            courts_rest = steps[-2:]
-            steps = steps[:-2]
+            steps = courts("v0", 0, (0, 1))
         else:
-            votes(t, "v%d" % t, (0, 1), [12, 13], lambda k: c1("rug", 32 * (t - 1) + k))
+            votes(t, "v%d" % t, (0, 1), [8, 9], lambda k: c1("rug", 32 * (t - 1) + k))
+            for a, b in others:
+                for s in rename(t - 1, a, b, A("res", RS * (t - 1), RS * (t - 1) + 480), A("okof", 32 + a // 16, 32 + b // 16)):
+                    s()
+            if t == 1:
+                end_constants()
             unpack2(t - 1, "q%d" % (t - 1))
             win = A("res", RS * (t - 1), RS * t)
             act(A("rug", 32 * t - 16, 32 * t), X(win, c1("ruof", 0)), IDT)
             for s in rename(t - 1, own[0], own[1], win, A("okof", 8 * me, 8 * me + 8)):
                 s()
             cp(A("offv"), X(A("name", *own), L_VO))
-            votes(t, "w%d" % t, (2, 3), [14, 15, 11], lambda k: c1("rug", 32 * t - 16 + k))
+            votes(t, "w%d" % t, (2, 3), [10, 11], lambda k: c1("rug", 32 * t - 16 + k))
             for a, b in others:
-                for s in rename(t - 1, a, b, win, A("okof", a // 16, b // 16)):
-                    s()
+                rename(t - 1, a, b, win, A("okof", a // 16, b // 16))[0]()
             steps = courts("v%d" % t, 0, (0, 1))
-        for s in steps:
+        for s in steps[:-1]:
             s()
+        later(steps[-1:])
         for b in range(4):
             hearing(t, b)
     t = RO - 1

from concourse.bass import DstId, RemoteDMATransfer
from concourse.mybir import AluOpType as ALU, AxisListType as AX, ActivationFunctionType as AF

W, RO, NR = 3584, 3, 4
WIN = 49152
BIGW = 65536.0
RND128 = 1610612736.0
RND2 = 25165824.0
RND4 = 50331652.0
RS = 960
SPLIT2 = True
START = 0
LP, LQ = 320, 800
OKB = (0, 160, 480, 640)

F, B, I, U = "float32", "bfloat16", "int32", "uint16"
SCRATCH = {
    "tab": ("sbuf", [128, WIN], B),
    "cli": ("sbuf", [128, 128], I), "tin": ("sbuf", [128, 288], F), "tout": ("sbuf", [128, 288], F),
    "ru0": ("sbuf", [128, 16], B), "rug": ("sbuf", [128, 96], B), "ruo": ("sbuf", [128, 16], B),
    "cu": ("sbuf", [128, 512], U), "ci": ("sbuf", [128, 512], I), "cj": ("sbuf", [128, 512], I),
    "name": ("sbuf", [128, 512], F), "base": ("sbuf", [128, 512], I), "bsel": ("sbuf", [128, 128], B),
    "ub": ("sbuf", [128, 512], B), "bit": ("sbuf", [128, 2048], B),
    "offv": ("sbuf", [128, 128], U), "eq": ("sbuf", [128, 2048], B), "ab": ("sbuf", [128, 640], B),
    "vt": ("sbuf", [128, 96], F), "res": ("sbuf", [128, RO * RS], B), "wi": ("sbuf", [128, 160], I),
    "wj": ("sbuf", [128, 480], I), "un": ("sbuf", [128, 320], B),
    "sc": ("sbuf", [128, 16], F), "pen": ("sbuf", [128, 32], F), "mm": ("sbuf", [128, 32], F),
    "selb": ("sbuf", [128, 8], F), "selu": ("sbuf", [128, 8], U), "selo": ("sbuf", [128, 256], F),
    "offs": ("sbuf", [128, 128], U), "offx": ("sbuf", [128, 32], F), "offy": ("sbuf", [128, 32], U),
    "okof": ("sbuf", [128, 64], U), "ruof": ("sbuf", [128, 4], U),
    "z": ("sbuf", [128, 512], B), "zs": ("sbuf", [128, 512], B), "ge": ("sbuf", [128, 512], B),
    "sn": ("sbuf", [128, 256], B), "d1": ("sbuf", [128, 512], B), "d2": ("sbuf", [128, 512], B),
    "ya": ("sbuf", [128, 512], B), "far": ("sbuf", [128, 512], B), "ua": ("sbuf", [128, 512], B),
    "junk": ("sbuf", [128, 1024], B), "junq": ("sbuf", [128, 128], F),
    "ss": ("sbuf", [128, 144], F), "nb": ("sbuf", [128, 16], F), "qq": ("sbuf", [128, 8], F),
    "sv": ("sbuf", [128, 32], F), "okt": ("sbuf", [128, 32], B),
    "pi": ("sbuf", [128, 16], I), "pc": ("sbuf", [128, 48], F), "col": ("sbuf", [128, 144], F),
    "ivw": ("sbuf", [128, 144], F), "ibo": ("sbuf", [128, 128], F), "ism": ("sbuf", [128, 64], F),
    "vw": ("sbuf", [128, 144], B), "bop": ("sbuf", [128, 128], B), "bon": ("sbuf", [128, 128], B),
    "idn": ("sbuf", [128, 128], B), "selp": ("sbuf", [128, 144], B), "ones": ("sbuf", [128, 128], B),
    "idx": ("sbuf", [128, 512], B), "jc": ("sbuf", [128, 64], B), "cf": ("sbuf", [128, 64], F),
    "lu": ("sbuf", [128, 64], U), "yco": ("sbuf", [128, 128], F),
    "pk": ("psum", [128, 512], F), "px0": ("psum", [128, 512], F), "px1": ("psum", [128, 512], F),
    "pv": ("psum", [128, 512], F),
}
MSGS = ["cl", "v0", "w0", "p0", "q0", "v1", "w1", "p1", "q1", "v2", "w2", "p2", "q2"]
DMAS = ["d_cl", "d_ru", "d_fa0", "d_fa1", "d_yf0", "d_yf1", "d_yc", "d_yr"]
SEMAPHORES = ["eV", "eS", "eP", "eG", "sent"] + ["m_" + m for m in MSGS] + DMAS


def msg_cols(m, r):
    if m == "cl":
        return "cu", 128 * r, 128 * r + 128
    t = int(m[1])
    if m[0] in "vw":
        a = 32 * t + (16 if m[0] == "w" else 0) + 4 * r
        return "vt", a, a + 4
    a = RS * t + (LP if m[0] == "p" else LQ) + 40 * r
    return "res", a, a + 36


def routes(T, topo):
    out = {}
    for r, c in enumerate(T.cores):
        direct, via, used = [], [], []
        for s, d in enumerate(T.cores):
            if s == r:
                continue
            if topo.may_write(c, d):
                direct.append(s)
                continue
            cand = [h for h in topo.cores_of(c) if h != c and h not in T.cores and h not in used and topo.may_write(h, d)]
            cand.sort(key=lambda h: topo.die(h) != topo.die(c))
            used.append(cand[0])
            via.append((cand[0], s))
        out[r] = (direct, via)
    return out


def mask_of(engs):
    m = 0
    for e in engs:
        m |= 1 << e
    return m


def helper_program(g, core, src, dst, T, topo, n_in):
    d = T.cores[dst]
    rid, pid = topo.addr(d, core)
    eng = topo.engines(core, d)
    for m in MSGS:
        buf, a, b = msg_cols(m, src)
        g.wait_ge(T.sem["m_" + m], n_in)
        g.remote_dma(T[buf][:, a:b], T[buf][:, a:b], T.sem["m_" + m], T.sem.sent, pid, rid, mask_of(eng))
    g.wait_ge(T.sem.sent, len(eng) * len(MSGS))


def rank_program(g, core, T, topo):
    rts = routes(T, topo)
    me = T.rank_of(core)
    if me is None:
        for r, (direct, via) in rts.items():
            far = topo.engines(T.cores[r], T.cores[direct[0]])
            for h, s in via:
                if h == core:
                    helper_program(g, core, r, s, T, topo, len(far))
        return
    rank_code(g, core, me, T, topo, rts)


def rank_code(g, core, me, T, topo, rts):
    ops = []

    def A(n, a=0, b=None, s=1, p=None):
        b = SCRATCH[n][1][1] if b is None else b
        ap = T[n][:, a:b:s] if s != 1 else T[n][:, a:b]
        if p is not None:
            ap = T[n][p[0]:p[1], a:b]
        if SCRATCH[n][0] == "psum":
            return (ap, [(n, 0, 1 << 20)])
        return (ap, [(n, a, b)])

    def X(w, o):
        return (w[0].indirect(o[0]), w[1], o[1])

    def rd(*xs):
        out = []
        for x in xs:
            if isinstance(x, tuple):
                out += x[1]
                if len(x) == 3:
                    out += x[2]
        return out

    def v(x):
        return x[0] if isinstance(x, tuple) else x

    def add(q, call, out, ins, ev=None):
        r = rd(*ins)
        w = []
        for o in out:
            w += o[1]
            if len(o) == 3:
                r += o[2]
        ops.append([q, call, r, w, ev])

    def ts(o, i, s1, op0, s2=None, op1=None):
        if op1 is None:
            add("V", lambda: g.vector.tensor_scalar(v(o), v(i), v(s1), None, op0), [o], [i, s1])
        else:
            add("V", lambda: g.vector.tensor_scalar(v(o), v(i), v(s1), v(s2), op0, op1), [o], [i, s1, s2])

    def tt(o, a, b, op):
        add("V", lambda: g.vector.tensor_tensor(v(o), v(a), v(b), op), [o], [a, b])

    def cp(o, i):
        add("V", lambda: g.vector.tensor_copy(v(o), v(i)), [o], [i])

    def ms(o, c):
        add("V", lambda: g.vector.memset(v(o), c), [o], [])

    def red(o, i, op, neg=False):
        add("V", lambda: g.vector.tensor_reduce(v(o), v(i), AX.X, op, negate=neg), [o], [i])

    def turn():
        add("V", lambda: g.vector.transpose(T.tout[:], T.tin[:]), [A("tout")], [A("tin")])

    def act(o, i, f, bias=0.0, scale=1.0, acc=None):
        outs = [o] + ([acc] if acc is not None else [])
        if acc is None:
            add("S", lambda: g.scalar.activation(v(o), v(i), f, bias=v(bias), scale=v(scale)), outs, [i, bias, scale])
        else:
            add("S", lambda: g.scalar.activation(v(o), v(i), f, bias=v(bias), scale=v(scale), accum_out=v(acc)),
                outs, [i, bias, scale])

    def mm(o, l, r, st, sp):
        add("P", lambda: g.tensor.matmul(v(o), v(l), v(r), st, sp), [o], [l, r])

    def iota(o, pat, base=0, cm=0, flt=True):
        if flt:
            add("G", lambda: g.iota(v(o), pat, base, cm, allow_small_or_imprecise_dtypes=True), [o], [])
        else:
            add("G", lambda: g.iota(v(o), pat, base, cm), [o], [])

    def dma(q, o, i, sem):
        eng = g.sync if q == "Y" else g.scalar
        add(q, lambda: eng.dma_start(v(o), v(i)), [o] if isinstance(o, tuple) else [], [i], ("dma", sem, 16))

    direct, via = rts[me]
    far = topo.engines(core, T.cores[direct[0]])
    n_sent = [0]

    def send(m):
        s = A(*msg_cols(m, me))
        trs = []
        for j, (h, _) in enumerate(via):
            spare = [e for e in topo.engines(core, h) if e not in far]
            eng = spare if j == 0 else far
            rid, pid = topo.addr(h, core)
            trs.append(RemoteDMATransfer(dst_ids=[DstId(rid=rid, pnc=pid)], dma_engine_mask=mask_of(eng[:len(far)]),
                                         remote_sem=T.sem["m_" + m], src=s[0], dst=s[0]))
            n_sent[0] += len(far)
        add("G", lambda: g.remote_dma_fused(trs, local_sem=T.sem.sent), [], [s], ("send",))
        for r in direct:
            rid, pid = topo.addr(T.cores[r], core)
            n_sent[0] += len(far)
            add("G", lambda rid=rid, pid=pid: g.remote_dma(s[0], s[0], T.sem["m_" + m], T.sem.sent, pid, rid, mask_of(far)),
                [], [s], ("send",))

    def arrive(m):
        w = [A(*msg_cols(m, r)) for r in range(NR) if r != me]
        add("X", None, w, [], ("ext", "m_" + m, len(far) * (NR - 1)))

    def c1(n, j):
        return A(n, j, j + 1)

    spare_work = []

    def later(steps):
        spare_work.extend(steps)

    def fill(n=1):
        for _ in range(n):
            if spare_work:
                spare_work.pop(0)()

    SIGN, IDT, ABS, RELU = AF.Sign, AF.Identity, AF.Abs, AF.Relu
    TAB = A("tab", 0, W)
    own = (128 * me, 128 * me + 128)
    others = [x for x in ((0, own[0]), (own[1], 512)) if x[1] > x[0]]

    dma("Y", A("cli"), T.cl[:], "d_cl")
    dma("S", A("ru0"), T.ru[:], "d_ru")
    half = W // 2
    dma("Y", A("tab", 0, half), T.fa[:, 0:half], "d_fa0")
    dma("S", A("tab", half, W), T.fa[:, half:W], "d_fa1")

    P_, p_, g_, h_, b_, x_, u_, e_, o_, y_ = [c1("pc", j) for j in range(10)]
    kap, g16, vo, so, jo, h16, t0, t1, t2, t3, t4, t5, t6, t7 = [c1("pc", j) for j in range(16, 30)]
    okA, okB, okL, ruA, ruB, ruL = [c1("pc", j) for j in range(32, 38)]
    ms(A("tin", 128, 144), 0.0)
    ms(A("tin", 272, 288), 0.0)
    ms(A("idx", p=(0, 64)), 0.0)
    iota(c1("pi", 0), [[0, 1]], 0, 1, False)
    iota(A("ism", 0, 8), [[32, 4], [160, 2]])
    iota(A("ism", 8, 16), [[0, 4], [-288, 2]], 144)
    iota(A("col"), [[1, 144]])
    iota(A("ivw"), [[1, 9], [0, 4], [1000, 4]], -3000)
    iota(A("ibo"), [[1, 8], [0, 16]])
    iota(A("ism", 16, 24), [[32, 4], [0, 2]])
    iota(A("ism", 24, 34), [[32, 5], [0, 2]], -16)
    iota(A("ism", 40, 56), [[-1, 4], [0, 4]], 3)
    for j, (sh, an) in enumerate(((0, 15), (4, 7), (4, 1), (0, 3), (2, 3), (3, 1), (0, 7), (0, 1), (1, 1))):
        ts(c1("pi", 1 + j), c1("pi", 0), sh, ALU.logical_shift_right, an, ALU.bitwise_and)
    cp(A("pc", 0, 10), A("pi", 0, 10))
    FF = A("cf", 0, 8)
    ts(FF, A("ism", 8, 16), h_, ALU.mult)
    ts(kap, b_, 4.0, ALU.mult, x_, ALU.add)
    ts(vo, e_, 16.0, ALU.mult, u_, ALU.add)
    tt(FF, FF, A("ism", 0, 8), ALU.add)
    L_FW, L_VO, L_OUT, L_YY, L_B5, L_B6, L_KP = (A("lu", 0, 8), A("lu", 8, 16), A("lu", 16, 24), A("lu", 24, 42),
                                                 A("lu", 42, 44), A("lu", 44, 52), A("lu", 52, 53))
    ts(L_VO, A("col", 0, 8), 2.0, ALU.mult, vo, ALU.add)
    ts(L_FW, FF, kap, ALU.add)
    ts(A("vw"), A("ivw"), g_, ALU.is_equal)
    ts(okA, b_, 1.0, ALU.is_equal, 160.0, ALU.mult)
    ts(okB, b_, y_, ALU.add, 160.0, ALU.mult)
    ts(t6, b_, 3.0, ALU.is_equal, 160.0, ALU.mult)
    ts(ruA, o_, LP + 32.0, ALU.add)
    ts(t7, b_, 3.0, ALU.is_equal, LQ - LP - 3.0, ALU.mult)
    tt(okL, okB, t6, ALU.add)
    ts(ruB, y_, float(LQ - LP), ALU.mult, ruA, ALU.add)
    ts(ruL, b_, LP + 32.0, ALU.add, t7, ALU.add)
    cp(A("tin", 0, 128), A("cli"))
    cp(A("tin", 144, 272), A("cli"))
    turn()
    cp(A("cu", *own), X(A("tout"), L_FW))
    send("cl")
    iota(A("idx", p=(0, 1)), [[128, 512]], -32768)
    cp(A("name", *own), A("cu", *own))
    cp(A("offv"), X(A("name", *own), L_VO))
    ms(A("vt", 4 * me + 3, 96, 16), 0.0)
    ms(A("res"), 0.0)

    def late_constants():
        ms(A("idx", p=(32, 33)), -255.0 * BIGW)
        ms(A("ones"), 1.0)
        ms(A("ss"), -0.5)
        ms(A("jc", 32, 64), -16640.0)
        ms(A("lu", 42, 46), 0)
        ts(g16, g_, 16.0, ALU.mult, 15.0, ALU.add)
        ts(jo, p_, -256.0, ALU.add)
        ts(t0, x_, 16.0, ALU.mult, b_, ALU.add)
        ts(t1, p_, 8.0, ALU.is_ge, 1.0, ALU.add)
        ts(t4, p_, 15.0, ALU.is_ge, 3.0, ALU.mult)
        ts(A("cf", 16, 32), A("ism", 40, 56), 0.25, ALU.mult)
        ts(A("cf", 32, 36), A("col", 0, 4), x_, ALU.is_equal)
        ts(so, t0, 12.0, ALU.add, 128.0, ALU.mult)
        ts(t2, p_, 12.0, ALU.is_ge, t1, ALU.add)
        ts(A("bop"), A("ibo"), g_, ALU.is_equal, BIGW, ALU.mult)
        ts(A("bon"), A("ibo"), g_, ALU.is_equal, -BIGW, ALU.mult)
        ts(A("idn"), A("col", 0, 128), P_, ALU.is_equal)
        ts(A("selp"), A("col"), g16, ALU.is_equal, 4096.0, ALU.mult)
        ts(A("jc", 0, 32), A("col", 0, 32), 16.0, ALU.mult, jo, ALU.add)
        ts(A("cf", 8, 16), A("col", 0, 8), 8192.0, ALU.mult, so, ALU.add)
        ts(t3, p_, 14.0, ALU.is_ge, t2, ALU.add)
        ms(A("lu", 46, 47), 1)
        ms(A("lu", 48, 51), 9)
        ms(A("ss", 9, 144, 16), 0.0)
        ts(A("lu", 51, 52), p_, 14.0, ALU.is_lt, 8.0, ALU.add)
        ms(A("cf", 40, 44), 0.0)
        ms(A("cf", 41, 42), 1.0)
        ms(A("cf", 43, 44), -3.0)
        ts(A("lu", 43, 44), t3, t4, ALU.add)
        ts(A("lu", 47, 48), t3, t4, ALU.add, 1.0, ALU.add)

    def end_constants():
        ts(h16, h_, 16.0, ALU.mult)
        ts(L_OUT, FF, p_, ALU.add)
        ts(A("ism", 16, 34), A("ism", 16, 34), h16, ALU.add, 0.0, ALU.max)
        cp(L_KP, kap)
        ts(L_YY, A("ism", 16, 34), 112.0, ALU.min, kap, ALU.add)

    PB = ["pk", "px0", "px1", "pv"]
    nstale = [0]

    def votes(t, m, blocks, on_s, ru):
        todo = [4 * kk + b for kk in range(3) for b in blocks]
        for j, k in enumerate(on_s):
            act(A("ab", 128 * j, 128 * j + 128), X(TAB, A("offv", 8 * k, 8 * k + 8)), ABS, ru(k), -1.0)
        j = 0
        while j < len(on_s):
            n = 1
            while j + n < len(on_s) and on_s[j + n] == on_s[j] + n:
                n += 1
            act(A("eq", 128 * on_s[j], 128 * (on_s[j] + n)), A("ab", 128 * j, 128 * (j + n)), RELU, 1.0, -1.0)
            j += n
        for k in todo:
            if k not in on_s:
                ts(A("eq", 128 * k, 128 * k + 128), X(TAB, A("offv", 8 * k, 8 * k + 8)), ru(k), ALU.is_equal)
        a = msg_cols(m, me)[1]
        for kk in (0, 2, 1):
            order = [b for b in range(max(blocks) + 1) if b not in blocks]
            order += [b for b in blocks if 4 * kk + b in on_s] + [b for b in blocks if 4 * kk + b not in on_s]
            for n, b in enumerate(order):
                k = 4 * kk + b
                mm(A(PB[kk], 0, 128), A("vw", 3 - b, 131 - b), A("eq", 128 * k, 128 * k + 128), n == 0, n == len(order) - 1)
            act(A("junk", 128 * kk, 128 * kk + 128), A(PB[kk], 0, 128), SIGN, -8.5, 1.0, c1("vt", a + kk))
        send(m)

    def courts(m, so_, blocks):
        t = int(m[1])
        return court_steps(m, so_, blocks, A("bit", 512 * t, 512 * t + 512))

    def court_steps(m, so_, blocks, bits):
        a = msg_cols(m, 0)[1]
        s0, s1, s2 = A("sc", 0, 16, 4), A("sc", 1, 16, 4), A("sc", 2, 16, 4)
        mx = [c1("mm", j) for j in range(3)]
        p0, p1, p2, u1, u2, u3 = [A("pen", 4 * j, 4 * j + 4) for j in range(6)]
        steps = [
            lambda: (arrive(m), tt(A("sc"), A("vt", a, a + 16), A("cf", 16, 32), ALU.add)),
            lambda: red(mx[0], s0, ALU.max),
            lambda: ts(p0, s0, mx[0], ALU.is_equal, -1536.0, ALU.mult),
            lambda: tt(u1, s1, p0, ALU.add),
            lambda: tt(u2, s2, p0, ALU.add),
            lambda: red(mx[1], u1, ALU.max),
            lambda: ts(p1, u1, mx[1], ALU.is_equal, -1024.0, ALU.mult),
            lambda: tt(u3, u2, p1, ALU.add),
            lambda: ts(A("selb"), A("cf", 8, 16), c1("pen", me), ALU.add, c1("pen", 4 + me), ALU.add),
            lambda: red(mx[2], u3, ALU.max),
            lambda: ts(c1("pen", 8), c1("pen", 20 + me), mx[2], ALU.is_equal, -512.0, ALU.mult),
            lambda: ts(A("selu"), A("selb"), c1("pen", 8), ALU.add, 1.0 / 128, ALU.mult),
        ]
        if so_:
            steps.append(lambda: cp(A("bsel"), X(bits, A("selu"))))
            steps.append(lambda: tt(A("selo", so_, so_ + 128), X(A("base"), A("selu")), A("bsel"), ALU.add))
        else:
            steps.append(lambda: cp(A("selo", 0, 128), X(A("name"), A("selu"))))
        for b in blocks:
            steps.append(lambda b=b: cp(A("offs", 32 * b, 32 * b + 32), A("selo", so_ + b, so_ + 128, 4)))
        return steps

    def court_lists(t):
        c40 = c1("mm", 21)
        steps = [
            lambda: ts(A("mm", 4, 7), A("mm", 0, 3), RND2, ALU.add, RND2, ALU.subtract),
            lambda: tt(A("mm", 8, 11), A("mm", 0, 3), A("mm", 4, 7), ALU.subtract),
            lambda: red(c1("mm", 12), A("mm", 8, 11), ALU.add, True),
            lambda: ts(c1("mm", 11), c1("mm", 12), 1.5, ALU.add),
            lambda: tt(A("mm", 16, 20), A("mm", 8, 12), A("cf", 32, 36), ALU.mult),
            lambda: red(c1("mm", 20), A("mm", 16, 20), ALU.add),
            lambda: ts(c40, c1("mm", 20), -160.0, ALU.mult, 120.0, ALU.add),
        ]
        last = t == RO - 1
        if not last:
            steps.append(lambda: ts(A("okof", 32, 64), A("col", 0, 32), c40, ALU.add, okA, ALU.add))
            steps.append(lambda: ts(c1("ruof", 2), c40, ruA, ALU.add))
        steps.append(lambda: ts(A("okof", 0, 32), A("col", 0, 32), c40, ALU.add, okL if last else okB, ALU.add))
        steps.append(lambda: ts(c1("ruof", 0), c40, ruL if last else ruB, ALU.add))
        return steps

    Z = A("z")
    JK = A("junk", 512, 1024)

    def count_v(q, w):
        ts(A("ge"), Z, q, ALU.add, float(w), ALU.is_ge)
        fill()
        add("V", lambda: g.vector.tensor_tensor_scan(T.sn[:], T.ge[:, 0:256], T.ge[:, 256:512], -256.0, ALU.add, ALU.add),
            [A("sn")], [A("ge")])

    def stale_levels(b):
        n = nstale[0]
        nstale[0] += 1
        win = A("ss", 16 * n, 16 * n + 16)
        for l in range(6):
            act(JK, A("zs"), SIGN, 0.0 if l == 0 else c1("nb", l), 1.0, c1("ss", 16 * n + l))
            if l < 5:
                act(A("junq", 0, 32), X(win, L_B5), SIGN, -0.5, -1.0, c1("nb", l + 1))
        act(A("junq"), X(win, L_B6), SIGN, -0.5, -1.0, c1("nb", 8 + b))

    def unpack2(t, m):
        arrive(m)
        src, dst = (LP, OKB[0]) if m[0] == "p" else (LQ, OKB[2])
        w = A("res", RS * t + src, RS * t + src + 160)
        act(A("un", 0, 160), w, ABS, -1.0)
        high = A("res", RS * t + dst + 160, RS * t + dst + 320)
        if m[0] == "p":
            act(A("un", 160, 320), w, RELU, -1.0)
        else:
            ts(high, w, 2.0, ALU.is_ge)
        act(A("res", RS * t + dst, RS * t + dst + 160), A("un", 0, 160), ABS, -1.0)
        if m[0] == "p":
            act(high, A("un", 160, 320), SIGN)

    def unpack3(t):
        arrive("p%d" % t)
        cp(A("wi"), A("res", RS * t + LP, RS * t + LP + 160))
        for b in range(3):
            ts(A("wj", 160 * b, 160 * b + 160), A("wi"), b, ALU.logical_shift_right, 1, ALU.bitwise_and)
        cp(A("res", RS * t, RS * t + 320), A("wj", 0, 320))
        cp(A("res", RS * t + OKB[2], RS * t + OKB[2] + 160), A("wj", 320, 480))

    def rename(t, a, b, win, lst):
        new = A("bit", 512 * (t + 1) + a, 512 * (t + 1) + b)
        return [lambda: tt(new, X(win, lst), A("bit", 512 * t + a, 512 * t + b), ALU.is_equal),
                lambda: tt(A("name", a, b), A("base", a, b), new, ALU.add)]

    def hearing(t, b):
        last = t == RO - 1
        off = A("offs", 32 * b, 32 * b + 32)
        R0 = RS * t
        px = A("px%d" % (b % 2), 0, 32)
        pk = A("pk")
        so_ = 128 if b >= 2 else 0
        if b != 2 or SPLIT2:
            act(A("z", 256, 512), X(TAB, A("offs", 32 * b + 16, 32 * b + 32)), IDT)
            cp(A("z", 0, 256), X(TAB, A("offs", 32 * b, 32 * b + 16)))
        else:
            act(A("zs"), X(TAB, A("offs", 32 * b + 32, 32 * b + 64)), IDT, -31.5)
            cp(Z, X(TAB, off))
        mm(pk, A("ones", p=(0, 64)), A("idx", p=(0, 64)), True, False)
        mm(px, A("idn"), A("jc", 0, 32), True, False)
        mm(px, A("idn"), A("jc", 32, 64), False, False)
        mm(pk, A("idn"), Z, False, False)
        sV, sS = c1("sn", 255), c1("sv", 0)
        if b == 0:
            q = -26.5
            for l, w in enumerate((27, 9, 3)):
                act(JK, Z, SIGN, q, 1.0, sS)
                count_v(q, w)
                if l < 2:
                    act(A("zs", 256 * l, 256 * l + 256), X(TAB, A("offs", 32 + 16 * l, 48 + 16 * l)), IDT, -31.5)
                bs, aV, aS, qn = c1("sv", 1), c1("sv", 2), c1("sv", 3), c1("sv", 8 + l)
                if l == 0:
                    bs = q - float(w + w // 3)
                else:
                    ts(bs, q, -float(w + w // 3), ALU.add)
                ts(aS, sS, 0.0, ALU.is_lt, float(w), ALU.mult)
                ts(aV, sV, 0.0, ALU.is_lt, float(w), ALU.mult)
                ts(qn, aS, aV, ALU.add, bs, ALU.add)
                q = qn
            qb = c1("sv", 4)
            if START == 0:
                later(courts("w%d" % t, 128, (2, 3)))
            fill()
            act(JK, Z, SIGN, q, 1.0, sS)
        else:
            q, qb = c1("qq", 2 * b), c1("qq", 2 * b + 1)
            ts(A("qq", 2 * b, 2 * b + 2), A("cf", 42, 44), c1("nb", 8 + b), ALU.add, 0.5, ALU.mult)
            act(JK, Z, SIGN, c1("nb", 8 + b), 2.0, sS)
            fill()
        if b == 0:
            ts(qb, q, -1.5, ALU.add)
        count_v(q, 1)
        fill()
        if b == 1:
            fill(len(spare_work) - 1)
            later(court_lists(t))
        if b == 1 or (b == 2 and SPLIT2):
            act(A("zs"), X(TAB, A("offs", 32 * b + 32, 32 * b + 64)), IDT, -31.5)
        nm = c1("sv", 6)
        ts(c1("sv", 5), sS, 0.0, ALU.is_lt, qb, ALU.add)
        fill()
        ts(nm, sV, 0.0, ALU.is_lt, c1("sv", 5), ALU.add)
        if b < 3:
            stale_levels(b + 1)
            if b == 0 and START == 1:
                later(courts("w%d" % t, 128, (2, 3)))
            fill()
            ts(A("d1"), Z, nm, ALU.add, 0.0, ALU.max)
            ts(A("d2"), Z, nm, ALU.add, 0.0, ALU.min)
            if b == 0 and START == 2:
                later(courts("w%d" % t, 128, (2, 3)))
            mm(pk, A("bop"), A("d1"), False, False)
            mm(pk, A("bon"), A("d2"), False, True)
        else:
            act(A("d1", 256, 512), A("z", 256, 512), ABS, nm)
            ts(A("d2", 0, 256), A("z", 0, 256), nm, ALU.add, 0.0, ALU.min)
            ts(A("d1", 0, 256), A("z", 0, 256), nm, ALU.add, 0.0, ALU.max)
            mm(A("pk", 0, 256), A("bon"), A("d2", 0, 256), False, False)
            mm(pk, A("bop"), A("d1"), False, True)
            if not last:
                unpack2(t, "p%d" % t)
                winA = A("res", R0, R0 + 480)
                act(A("rug", 32 * t, 32 * t + 16), X(winA, c1("ruof", 2)), IDT)
        fill(3)
        key, tq = c1("sv", 12), c1("sv", 13)
        red(key, pk, ALU.min)
        if b == 3 and not last:
            later(rename(t, own[0], own[1], winA, A("okof", 32 + 8 * me, 40 + 8 * me)) + [lambda: cp(A("offv"), X(A("name", *own), L_VO))])
        fill()
        ts(tq, key, RND128, ALU.add, RND128, ALU.subtract)
        if b < 3:
            fill()
        inp = b <= (2 if last else 1)
        j = b if inp else b - (3 if last else 2)
        slot = R0 + (LP if inp else LQ) + 40 * me
        rc = slot + 32 + j
        ts(A("ya"), Z, tq, ALU.add, key, ALU.subtract)
        ts(A("res", rc, rc + 2), A("cf", 40, 42), key, ALU.add, tq, ALU.subtract)
        ts(A("far"), A("ya"), RND4, ALU.add, RND4, ALU.not_equal)
        for p in range(16):
            mm(px, A("selp", 15 - p, 143 - p), A("far", p, 512, 16), False, p == 15)
        word = A("res", slot, slot + 32)
        closes = b == 3 or b == (2 if last else 1)
        if b == 3:
            act(A("ua"), A("ya"), SIGN, 0.0, -1.0)
            fill(3)
        else:
            ts(A("ua"), Z, 1.0, ALU.add, c1("res", rc), ALU.min)
            ts(A("ub"), Z, c1("res", rc + 1), ALU.subtract, 0.0, ALU.max)
            fill()
        if last and b == 3:
            ts(word, px, 0.0, ALU.is_lt)
            send("q%d" % t)
        tt(A("offx"), px, A("selo", so_ + b, so_ + 128, 4), ALU.max)
        if last and b == 3:
            pass
        elif j == 0:
            ts(word, px, 0.0, ALU.is_lt)
        else:
            ts(A("okt"), px, 0.0, ALU.is_lt, float(2 ** j), ALU.mult)
        cp(A("offy"), A("offx"))
        if j > 0:
            tt(word, word, A("okt"), ALU.add)
            if closes:
                send(("p%d" if inp else "q%d") % t)
        else:
            fill()
        tt(X(A("tab"), A("offy")), Z if b == 3 else A("ub"), A("ua"), ALU.add)
        fill(1 if b < 2 else len(spare_work))

    for t in range(RO):
        if t == 0:
            votes(0, "v0", (0, 1), [8, 9], lambda k: c1("ru0", 4 * (k % 4) + k // 4))
            votes(0, "w0", (2, 3), [10, 11], lambda k: c1("ru0", 4 * (k % 4) + k // 4))
            late_constants()
            arrive("cl")
            for a, b in others:
                cp(A("name", a, b), A("cu", a, b))
            cp(A("ci"), A("cu"))
            ts(A("cj"), A("ci"), 1, ALU.bitwise_and)
            ts(A("base"), A("ci"), 4094, ALU.bitwise_and)
            cp(A("bit", 0, 512), A("cj"))
            steps = courts("v0", 0, (0, 1))
        else:
            votes(t, "v%d" % t, (0, 1), [8, 9], lambda k: c1("rug", 32 * (t - 1) + k))
            for a, b in others:
                for s in rename(t - 1, a, b, A("res", RS * (t - 1), RS * (t - 1) + 480), A("okof", 32 + a // 16, 32 + b // 16)):
                    s()
            if t == 1:
                end_constants()
            unpack2(t - 1, "q%d" % (t - 1))
            win = A("res", RS * (t - 1), RS * t)
            act(A("rug", 32 * t - 16, 32 * t), X(win, c1("ruof", 0)), IDT)
            for s in rename(t - 1, own[0], own[1], win, A("okof", 8 * me, 8 * me + 8)):
                s()
            cp(A("offv"), X(A("name", *own), L_VO))
            votes(t, "w%d" % t, (2, 3), [10, 11], lambda k: c1("rug", 32 * t - 16 + k))
            for a, b in others:
                rename(t - 1, a, b, win, A("okof", a // 16, b // 16))[0]()
            steps = courts("v%d" % t, 0, (0, 1))
        for s in steps[:-1]:
            s()
        later(steps[-1:])
        for b in range(4):
            hearing(t, b)
    t = RO - 1
    dma("Y", T.yf[:, 0:half], A("tab", 0, half), "d_yf0")
    dma("S", T.yf[:, half:W], A("tab", half, W), "d_yf1")
    unpack3(t)
    arrive("q%d" % t)
    win = A("res", RS * t, RS * t + RS)
    RU = A("rug", 32 * t, 32 * t + 16)
    act(RU, X(win, c1("ruof", 0)), IDT)
    act(A("ruo"), X(RU, L_KP), IDT)
    dma("S", T.yr[:], A("ruo"), "d_yr")
    for s in rename(t, own[0], own[1], win, A("okof", 8 * me, 8 * me + 8)):
        s()
    cp(A("tin"), X(A("name", *own), L_YY))
    turn()
    cp(A("yco"), X(A("tout"), L_OUT))
    dma("Y", T.yc[:], A("yco"), "d_yc")
    emit(g, T, ops, n_sent[0])


def emit(g, T, ops, n_sent):
    hist = {}
    clock = {q: {} for q in "VSPGY"}
    done = []
    waits = []
    marked = set()
    for n, (q, call, rds, wrs, ev) in enumerate(ops):
        key = q if ev is None else (None if ev[0] == "send" else ev[1])
        need = []
        if q != "X":
            for (buf, a, b), wr in [(x, False) for x in rds] + [(x, True) for x in wrs]:
                psum = SCRATCH[buf][0] == "psum"
                for (m, a2, b2, w2) in hist.get(buf, []):
                    if a2 < b and a < b2 and (wr or w2 or psum):
                        same = ops[m][0] == q and ops[m][4] is None
                        if same and (q == "P" or not (wr or w2)):
                            continue
                        if ops[m][4] is not None and ops[m][4][0] == "send":
                            continue
                        need.append(m)
        ws = []
        ck = clock.get(q, {})
        for m in sorted(set(need), reverse=True):
            km = done[m][0]
            if ck.get(km, -1) >= m:
                continue
            ws.append(m)
            marked.add(m)
            for k2, v2 in done[m][1].items():
                if ck.get(k2, -1) < v2:
                    ck[k2] = v2
        snap = dict(ck)
        snap[key] = n
        done.append((key, snap))
        waits.append(ws)
        for x in wrs:
            if q != "X":
                hist[x[0]] = [e for e in hist.get(x[0], []) if not (x[1] <= e[1] and e[2] <= x[2])]
            hist.setdefault(x[0], []).append((n, x[1], x[2], True))
        for x in rds:
            hist.setdefault(x[0], []).append((n, x[1], x[2], False))
    queue = {"V": g.vector, "S": g.scalar, "P": g.tensor, "G": g, "Y": g.sync}
    count = {q: 0 for q in "VSPG"}
    value = {}
    for n, (q, call, rds, wrs, ev) in enumerate(ops):
        if ev is not None and ev[0] != "send":
            value[n] = (ev[1], ev[2])
        elif n in marked:
            count[q] += 1
            value[n] = ("e" + q, count[q])
        if q == "X":
            continue
        for m in waits[n]:
            queue[q].wait_ge(T.sem[value[m][0]], value[m][1])
        ins = call()
        if ev is not None and ev[0] == "dma":
            ins.then_inc(T.sem[ev[1]], 16)
        elif n in marked:
            ins.then_inc(T.sem["e" + q], 1)
    for d in DMAS:
        g.wait_ge(T.sem[d], 16)
    for q in "VSPG":
        g.wait_ge(T.sem["e" + q], count[q])
    g.wait_ge(T.sem.sent, n_sent)
